import numpy as np
import ml_dtypes


def mxq(x, axis, fmt="e4m3"):
    dtype, down = {"e4m3": (ml_dtypes.float8_e4m3fn, 7), "e5m2": (ml_dtypes.float8_e5m2, 14)}[fmt]
    v = np.moveaxis(np.asarray(x, np.float32).astype(ml_dtypes.bfloat16).astype(np.float64), axis, -1)
    blocks = v.reshape(v.shape[:-1] + (-1, 32))
    amax = np.abs(blocks).max(-1, keepdims=True)
    byte = np.maximum(np.where(amax > 0, np.frexp(amax)[1] - 1 + 127, 0) - down, 1)
    scale = np.exp2(byte - 127.0)
    codes = (blocks / scale).astype(np.float32).astype(dtype).astype(np.float64)
    return np.moveaxis((codes * scale).reshape(v.shape), -1, axis)


WIDE = False


def mx_kscale(k):
    if not WIDE:
        return np.ones(k)
    levels = np.array([10, -10, 5, -5, 0])
    if k % 512:
        return np.exp2(np.random.permutation(np.resize(levels, k // 32))).repeat(32)
    a = np.empty((k // 512, 16))
    for p in range(k // 512):
        a[p, :8] = np.random.permutation(np.resize(levels, 8))
        for g in range(8):
            far = levels[np.abs(levels - a[p, g]) >= 10]
            a[p, g + 8] = far[np.random.randint(len(far))]
    return np.exp2(a.ravel()).repeat(32)


BF16 = ml_dtypes.bfloat16


def bf(x):
    return np.asarray(x, np.float32).astype(BF16)


def f64(x):
    return np.asarray(x).astype(np.float64)


E2M1 = np.array([0.0, 0.5, 1.0, 1.5, 2.0, 3.0, 4.0, 6.0, -0.0, -0.5, -1.0, -1.5, -2.0, -3.0, -4.0, -6.0])


def pack_weight(w, fmt):
    k, n = w.shape
    w = f64(bf(w)).reshape(k // 32, 32, n)
    amax = np.abs(w).max(1)
    if fmt == "e4m3":
        byte = np.frexp(amax)[1] - 1 + 127 - 7
    else:
        mant, ex = np.frexp(amax / 6.0)
        byte = np.where(mant > 0.5, ex, ex - 1) + 127
    byte = np.clip(np.where(amax > 0, byte, 1), 1, 254)
    scaled = (w * np.exp2(127.0 - byte)[:, None, :]).reshape(k, n).astype(np.float32)
    by_word = np.ascontiguousarray(scaled.reshape(k // 512, 128, 4, n).transpose(0, 1, 3, 2))
    if fmt == "e4m3":
        words = by_word.astype(ml_dtypes.float8_e4m3fn).view(np.uint8)
    else:
        c = by_word.astype(ml_dtypes.float4_e2m1fn).view(np.uint8) & 0xF
        words = c[..., 0::2] | (c[..., 1::2] << 4)
    return np.ascontiguousarray(words), np.ascontiguousarray(byte.astype(np.uint8).reshape(k // 512, 16, n))


def unpack_weight(words, scales, fmt):
    g, p, n, _ = words.shape
    if fmt == "e4m3":
        vals = np.ascontiguousarray(words).view(ml_dtypes.float8_e4m3fn).astype(np.float64)
    else:
        nib = np.empty((g, p, n, 4), np.uint8)
        nib[..., 0::2] = words & 0xF
        nib[..., 1::2] = words >> 4
        vals = E2M1[nib]
    vals = vals * np.repeat(np.exp2(scales.astype(np.float64) - 127.0), 8, axis=1)[..., None]
    return vals.transpose(0, 1, 3, 2).reshape(g * 512, n)
def pack4(w):
    words, scales = pack_weight(w, "e2m1")
    return words.reshape(words.shape[0], 128, -1), scales


def unpack4(words, scales):
    return unpack_weight(words.reshape(words.shape[0], 128, -1, 2), scales, "e2m1")


def planes(Y):
    n, m = Y.shape
    b = f64(bf(Y)).reshape(n // 32, 32, m)
    amax = np.abs(b).max(1)
    byte = np.clip(np.where(amax > 0, np.frexp(amax)[1] - 1 + 127 - 7, 1), 1, 254)
    codes = (b * np.exp2(127.0 - byte)[:, None, :]).reshape(n, m).astype(np.float32).astype(ml_dtypes.float8_e4m3fn).view(np.uint8)
    words = codes.reshape(n // 512, 128, 4, m).transpose(0, 1, 3, 2)
    return np.ascontiguousarray(words), np.ascontiguousarray(byte.astype(np.uint8).reshape(n // 512, 16, m))


M, P, N, O = 1024, 1024, 1024, 512


def pseudo_derivative(v):
    return 0.3 * np.maximum(0.0, 1.0 - np.abs(v - 1.0))


def setup_inputs():
    s, r = mx_kscale(P), mx_kscale(O)
    t = mx_kscale(M)
    z = bf(np.random.standard_normal((M, P)) * s)
    v0 = bf(np.random.standard_normal((M, N)))
    wrec_words, wrec_scales = pack4(np.random.standard_normal((P, N)) / np.sqrt(P) / s[:, None])
    err = bf(np.random.standard_normal((M, O)) * 2.0 * r * t[:, None])
    bfb_words, bfb_scales = pack4(np.random.standard_normal((O, N)) / np.sqrt(O) / r[:, None])
    zbar = bf(np.random.standard_normal((M, P)) / np.sqrt(M) / t[:, None])
    return {
        "z": z,
        "v0": v0,
        "wrec_words": wrec_words,
        "wrec_scales": wrec_scales,
        "err": err,
        "bfb_words": bfb_words,
        "bfb_scales": bfb_scales,
        "zbar": zbar,
    }


def core(z, v0, wrec_words, wrec_scales, err, bfb_words, bfb_scales, zbar):
    v = 0.8 * f64(v0) + (mxq(f64(z), 1, "e4m3") @ unpack4(wrec_words, wrec_scales))
    psi = pseudo_derivative(v)
    l = mxq(f64(err), 1, "e4m3") @ unpack4(bfb_words, bfb_scales)
    d = l * psi
    return mxq(f64(zbar), 0, "e4m3").T @ mxq(d, 0, "e4m3")


def reference(z, v0, wrec_words, wrec_scales, err, bfb_words, bfb_scales, zbar):
    R_out = core(z, v0, wrec_words, wrec_scales, err, bfb_words, bfb_scales, zbar)
    words, scales = planes(R_out)
    return R_out, words, scales

@@ -1,0 +1,529 @@
+from contextlib import ExitStack
+
+import concourse.mybir as mybir
+from concourse.masks import make_identity
+
+M, PRE, N, O = 1024, 1024, 1024, 512
+FLOPS = 2 * M * N * (PRE + O + PRE)
+
+F32 = mybir.dt.float32
+BF16 = mybir.dt.bfloat16
+I32 = mybir.dt.int32
+U32 = mybir.dt.uint32
+U8 = mybir.dt.uint8
+FP8X4 = mybir.dt.float8_e4m3fn_x4
+FP4X4 = mybir.dt.float4_e2m1fn_x4
+ALU = mybir.AluOpType
+ACT = mybir.ActivationFunctionType
+
+P = 128
+
+
+def tile_epropeligibilityweightupdate_x2_kernel(
+    tc, z, v0, wrec_words, wrec_scales, err, bfb_words, bfb_scales, zbar, out_0, out_1, out_2
+):
+    nc = tc.nc
+    with ExitStack() as ctx:
+        keep = ctx.enter_context(tc.tile_pool(name="keep", bufs=1))
+        stage = ctx.enter_context(tc.tile_pool(name="stage", bufs=1))
+        wide = ctx.enter_context(tc.tile_pool(name="wide", bufs=4))
+        psum = ctx.enter_context(tc.psum_pool(name="psum", bufs=1))
+        ctx.enter_context(tc.manual_schedule())
+
+        ident = keep.tile([P, P], F32, name="ident")
+        z_sb = keep.tile([P, 2, 4, PRE], BF16, name="z_sb", align_bytes=64)
+        e_sb = keep.tile([P, 2, 4, O], BF16, name="e_sb", align_bytes=64)
+        v_sb = keep.tile([P, 2, 4, N], BF16, name="v_sb", align_bytes=64)
+        zb_sb = keep.tile([P, 2, 4, PRE], BF16, name="zb_sb", align_bytes=64)
+        w_words = keep.tile([P, 2, 2 * N], U8, name="w_words", align_bytes=64)
+        b_words = keep.tile([P, 2 * N], U8, name="b_words", align_bytes=64)
+        w_scales = keep.tile([P, 2, N], U8, name="w_scales", align_bytes=64)
+        b_scales = keep.tile([P, N], U8, name="b_scales", align_bytes=64)
+        z_codes = keep.tile([P, 2, 4, 2 * P], U32, name="z_codes", align_bytes=64)
+        z_scales = keep.tile([P, 2, 4, 2 * P], U8, name="z_scales", align_bytes=64)
+        e_codes = keep.tile([P, 2, 4 * P], U32, name="e_codes", align_bytes=64)
+        e_scales = keep.tile([P, 2, 4 * P], U8, name="e_scales", align_bytes=64)
+        zb_codes = keep.tile([P, 2, PRE], U32, name="zb_codes", align_bytes=64)
+        zb_scales = keep.tile([P, 2, PRE], U8, name="zb_scales", align_bytes=64)
+        d_codes = keep.tile([P, 2, N], U32, name="d_codes", align_bytes=64)
+        d_scales = keep.tile([P, 2, N], U8, name="d_scales", align_bytes=64)
+        o_f32 = keep.tile([P, 2, 4, N], F32, name="o_f32", align_bytes=64)
+        o_codes = keep.tile([P, 2, N], U32, name="o_codes", align_bytes=64)
+        o_scales = keep.tile([P, 2, N], U8, name="o_scales", align_bytes=64)
+        warm = keep.tile([P, 16], F32, name="warm")
+
+        def rows(x, g):
+            return x[512 * g : 512 * (g + 1), :].rearrange("(p t) c -> p t c", t=4)
+
+        def copy(eng, out, in_):
+            if eng == "S":
+                nc.scalar.copy(out=out, in_=in_)
+            elif eng == "V":
+                nc.vector.tensor_copy(out=out, in_=in_)
+            else:
+                nc.gpsimd.tensor_scalar(out=out, in0=in_, scalar1=1.0, scalar2=0.0, op0=ALU.mult, op1=ALU.add)
+
+        live = {}
+        count = {}
+
+        def ring(pool, name, depth, shape, dtype, **kw):
+            n = count.get(name, 0)
+            count[name] = n + 1
+            return pool.tile(shape, dtype, name="%s%d" % (name, n % depth), **kw)
+
+        def setup():
+            nc.vector.memset(w_scales[:].rearrange("p c n -> p (c n)").bitcast(I32), 0)
+            nc.vector.memset(b_scales[:].bitcast(I32), 0)
+            nc.vector.memset(warm[:, 0:1], 0.0)
+            nc.scalar.activation(out=warm[:, 8:9], in_=warm[:, 0:1], func=ACT.Abs)
+
+        def mkident():
+            make_identity(nc, ident[:])
+
+        def queue(eng):
+            return {"S": nc.scalar, "G": nc.gpsimd, "Y": nc.sync}[eng]
+
+        def ld_z(g, t0, t1):
+            nc.sync.dma_start(out=z_sb[:, g, t0:t1, :], in_=rows(z, g)[:, t0:t1, :])
+
+        def ld_e(g):
+            nc.sync.dma_start(out=e_sb[:, g, :, :], in_=rows(err, g))
+
+        def ld_v(g, h, t0, t1):
+            nc.sync.dma_start(out=v_sb[:, g, t0:t1, 512 * h : 512 * (h + 1)], in_=rows(v0, g)[:, t0:t1, 512 * h : 512 * (h + 1)])
+
+        def ld_zb(g):
+            nc.sync.dma_start(out=zb_sb[:, g, :, :], in_=rows(zbar, g))
+
+        def ld_w(h):
+            b = slice(N * h, N * (h + 1))
+            nc.sync.dma_start(out=w_words[:, :, b].bitcast(I32), in_=wrec_words.rearrange("c p b -> p c b")[:, :, b].bitcast(I32))
+
+        def ld_b():
+            nc.sync.dma_start(out=b_words[:].bitcast(I32), in_=bfb_words[0].bitcast(I32))
+
+        def ld_ws(eng, q):
+            if True:
+                queue(eng).dma_start(
+                    out=w_scales[32 * q : 32 * q + 4, :, :].bitcast(I32),
+                    in_=wrec_scales[:, 4 * q : 4 * q + 4, :].rearrange("c r n -> r c n").bitcast(I32),
+                )
+
+        def ld_bs(eng, q):
+            if True:
+                queue(eng).dma_start(
+                    out=b_scales[32 * q : 32 * q + 4, :].bitcast(I32),
+                    in_=bfb_scales[0, 4 * q : 4 * q + 4, :].bitcast(I32),
+                )
+
+        def turn(key, sources):
+            bank = ring(psum, "bank", 8, [P, 512], F32)
+            for a, words in enumerate(sources):
+                for u in range(2):
+                    j = 2 * a + u
+                    nc.tensor.transpose(bank[:, P * j : P * (j + 1)], words[:, u : 2 * P : 2], ident[:])
+            live[key] = bank
+
+        def tz(g, t):
+            words = z_sb[:, g, t, :].bitcast(F32)
+            turn(("z", g, t), [words[:, 256 * c : 256 * (c + 1)] for c in range(2)])
+
+        def te(g, j):
+            turn(("e", g, j), [e_sb[:, g, 2 * j + a, :].bitcast(F32) for a in range(2)])
+
+        def tcopy(eng, kind, g, j):
+            bank = live.pop((kind, g, j))
+            turned = ring(stage, "turned", 6, [P, 1024], BF16, align_bytes=64)
+            copy(eng, turned[:].bitcast(F32).rearrange("p (a m u) -> p a m u", a=2, u=2),
+                 bank[:].rearrange("p (a u m) -> p a m u", a=2, u=2))
+            live[("t", kind, g, j)] = turned
+
+        def tq(kind, g, j):
+            turned = live.pop(("t", kind, g, j))
+            if kind == "z":
+                codes, scales = z_codes[:, g, j, :], z_scales[:, g, j, :]
+            else:
+                codes, scales = e_codes[:, g, 256 * j : 256 * (j + 1)], e_scales[:, g, 256 * j : 256 * (j + 1)]
+            nc.vector.quantize_mx(out=codes.bitcast(FP8X4), scales=scales, in_=turned[:])
+
+        def mz(g, h, t):
+            bank = ring(psum, "bank", 8, [P, 512], F32)
+            for c in range(2):
+                nc.tensor.matmul_mx(
+                    out=bank[:],
+                    lhsT=z_codes[:, g, t, P * c : P * (c + 1)].bitcast(FP8X4),
+                    lhsT_scale=z_scales[:, g, t, P * c : P * (c + 1)],
+                    rhs=w_words[:, c, N * h : N * (h + 1)].bitcast(FP4X4),
+                    rhs_scale=w_scales[:, c, 512 * h : 512 * (h + 1)],
+                    start=(c == 0), stop=(c == 1))
+            live[("zw", g, h, t)] = bank
+
+        def addv(g, h, t):
+            bank = live.pop(("zw", g, h, t))
+            if ("v", g, h) not in live:
+                live[("v", g, h)] = wide.tile([P, 4, 512], F32, name="v_f32", align_bytes=64)
+            nc.vector.scalar_tensor_tensor(
+                out=live[("v", g, h)][:, t, :], in0=v_sb[:, g, t, 512 * h : 512 * (h + 1)], scalar=0.8,
+                in1=bank[:], op0=ALU.mult, op1=ALU.add)
+
+        def dist(g, h, t):
+            nc.scalar.activation(out=live[("v", g, h)][:, t, :], in_=live[("v", g, h)][:, t, :], func=ACT.Abs, bias=-1.0, scale=1.0)
+
+        def ramp(eng, g, q):
+            src = live[("v", g, q // 4)][:, :, P * (q % 4) : P * (q % 4 + 1)].rearrange("p t n -> p n t")
+            w = ring(stage, "ramp", 6, [P, P, 4], F32, align_bytes=64)
+            if eng == "S":
+                nc.scalar.activation(out=w[:], in_=src, func=ACT.Identity, bias=0.3, scale=-0.3)
+            else:
+                (nc.vector if eng == "V" else nc.gpsimd).tensor_scalar(
+                    out=w[:], in0=src, scalar1=-0.3, scalar2=0.3, op0=ALU.mult, op1=ALU.add)
+            live[("w", g, q)] = w
+
+        def ml(g, q):
+            bank = ring(psum, "bank", 8, [P, 512], F32)
+            for t in range(4):
+                nc.tensor.matmul_mx(
+                    out=bank[:, P * t : P * (t + 1)],
+                    lhsT=e_codes[:, g, P * t : P * (t + 1)].bitcast(FP8X4),
+                    lhsT_scale=e_scales[:, g, P * t : P * (t + 1)],
+                    rhs=b_words[:, 2 * P * q : 2 * P * (q + 1)].bitcast(FP4X4),
+                    rhs_scale=b_scales[:, P * q : P * (q + 1)],
+                    start=True, stop=True)
+            live[("l", g, q)] = bank
+
+        def gate(g, q):
+            bank = live.pop(("l", g, q))
+            d = ring(stage, "d_bf", 8, [P, P, 4], BF16, align_bytes=64)
+            nc.vector.scalar_tensor_tensor(
+                out=d[:], in0=live.pop(("w", g, q))[:], scalar=0.0,
+                in1=bank[:].rearrange("p (t n) -> p n t", t=4), op0=ALU.max, op1=ALU.mult)
+            live[("d", g, q)] = d
+
+        def dq(g, q, q1):
+            nc.vector.quantize_mx(
+                out=d_codes[:, g, P * q : P * (q + 1)].bitcast(FP8X4), scales=d_scales[:, g, P * q : P * (q + 1)],
+                in_=live.pop(("d", g, q))[:].rearrange("p n t -> p (n t)"))
+
+        def zbc(eng, g, i, s0, s1):
+            if ("zb", g, i) not in live:
+                live[("zb", g, i)] = wide.tile([P, 4, P, 4], BF16, name="zb_grouped", align_bytes=64)
+            copy(eng, live[("zb", g, i)][:, s0:s1, :, :],
+                 zb_sb[:, g, :, 512 * i : 512 * (i + 1)].rearrange("p t (m s) -> p s m t", s=4)[:, s0:s1, :, :])
+
+        def zbq(g, i):
+            nc.vector.quantize_mx(
+                out=zb_codes[:, g, 512 * i : 512 * (i + 1)].bitcast(FP8X4), scales=zb_scales[:, g, 512 * i : 512 * (i + 1)],
+                in_=live.pop(("zb", g, i))[:].rearrange("p s m t -> p (s m t)"))
+
+        def mo(i, q):
+            bank = ring(psum, "bank", 8, [P, 512], F32)
+            for s in range(4):
+                c = slice(512 * i + P * s, 512 * i + P * (s + 1))
+                for g in range(2):
+                    nc.tensor.matmul_mx(
+                        out=bank[:, P * s : P * (s + 1)],
+                        lhsT=zb_codes[:, g, c].bitcast(FP8X4), lhsT_scale=zb_scales[:, g, c],
+                        rhs=d_codes[:, g, P * q : P * (q + 1)].bitcast(FP8X4), rhs_scale=d_scales[:, g, P * q : P * (q + 1)],
+                        start=(g == 0), stop=(g == 1))
+            live[("o", i, q)] = bank
+
+        def ocopy(eng, i, q):
+            copy(eng, o_f32[:, i, :, P * q : P * (q + 1)], live[("o", i, q)][:].rearrange("p (s n) -> p s n", s=4))
+
+        def oround(eng, i, q):
+            ob = ring(stage, "o_bf", 8, [P, P, 4], BF16, align_bytes=64)
+            if eng != "V":
+                copy("S" if eng == "S" else "V", ob[:], live[("o", i, q)][:].rearrange("p (s n) -> p n s", s=4))
+            else:
+                copy(eng, ob[:], o_f32[:, i, :, P * q : P * (q + 1)].rearrange("p s n -> p n s"))
+            live[("ob", i, q)] = ob
+
+        def oq(i, q, q1):
+            nc.vector.quantize_mx(
+                out=o_codes[:, i, P * q : P * (q + 1)].bitcast(FP8X4), scales=o_scales[:, i, P * q : P * (q + 1)],
+                in_=live.pop(("ob", i, q))[:].rearrange("p n s -> p (n s)"))
+
+        def st_f(eng, i, q0, q1):
+            c = slice(P * q0, P * q1)
+            queue(eng).dma_start(out=rows(out_0, i)[:, :, c], in_=o_f32[:, i, :, c])
+
+        def st_c(eng, q0, q1):
+            c = slice(P * q0, P * q1)
+            queue(eng).dma_start(
+                out=out_1.rearrange("g p m t -> p g (m t)").bitcast(I32)[:, :, c], in_=o_codes[:, :, c].bitcast(I32))
+
+        def st_s(eng, q):
+            queue(eng).dma_start(
+                out=out_2[:, 4 * q : 4 * q + 4, :].rearrange("g r n -> r g n").bitcast(I32),
+                in_=o_scales[32 * q : 32 * q + 4, :, :].bitcast(I32))
+
+        setup()
+        mkident()
+        ld_z(0,0,1)
+        tz(0,0)
+        tcopy('V','z',0,0)
+        tq('z',0,0)
+        ld_z(0,1,2)
+        tz(0,1)
+        ld_z(0,3,4)
+        ld_ws('S',2)
+        tz(0,3)
+        ld_ws('S',3)
+        tcopy('V','z',0,1)
+        ld_ws('S',1)
+        ld_bs('G',3)
+        ld_ws('S',0)
+        ld_z(0,2,3)
+        tcopy('S','z',0,3)
+        tz(0,2)
+        ld_w(0)
+        tq('z',0,1)
+        tq('z',0,3)
+        tcopy('V','z',0,2)
+        tq('z',0,2)
+        ld_v(0,0,0,2)
+        mz(0,0,0)
+        addv(0,0,0)
+        dist(0,0,0)
+        mz(0,0,1)
+        addv(0,0,1)
+        mz(0,0,3)
+        ld_bs('G',1)
+        mz(0,0,2)
+        ld_v(0,0,2,4)
+        ld_e(0)
+        te(0,0)
+        addv(0,0,2)
+        ld_z(1,2,4)
+        ld_e(1)
+        tz(1,2)
+        addv(0,0,3)
+        tcopy('V','z',1,2)
+        dist(0,0,1)
+        te(0,1)
+        ld_z(1,0,2)
+        tcopy('V','e',0,1)
+        tq('z',1,2)
+        dist(0,0,2)
+        tcopy('S','e',0,0)
+        tq('e',0,1)
+        tz(1,3)
+        te(1,1)
+        tcopy('V','e',1,1)
+        tq('e',0,0)
+        tcopy('S','z',1,3)
+        te(1,0)
+        dist(0,0,3)
+        tq('z',1,3)
+        ramp('V',0,3)
+        ld_bs('G',0)
+        ld_bs('G',2)
+        ramp('G',0,0)
+        tcopy('S','e',1,0)
+        tq('e',1,0)
+        tq('e',1,1)
+        ramp('G',0,1)
+        tz(1,0)
+        tcopy('S','z',1,0)
+        tq('z',1,0)
+        tz(1,1)
+        tcopy('S','z',1,1)
+        tq('z',1,1)
+        ld_zb(0)
+        zbc('S',0,1,2,4)
+        zbc('S',0,0,0,2)
+        zbc('V',0,0,2,4)
+        ld_v(1,0,0,4)
+        mz(1,0,3)
+        addv(1,0,3)
+        mz(1,0,0)
+        addv(1,0,0)
+        dist(1,0,0)
+        dist(1,0,3)
+        mz(1,0,2)
+        mz(1,0,1)
+        addv(1,0,2)
+        dist(1,0,2)
+        ld_b()
+        ld_w(1)
+        ml(0,1)
+        ml(0,3)
+        ml(0,0)
+        mz(0,1,3)
+        addv(1,0,1)
+        dist(1,0,1)
+        ld_zb(1)
+        zbc('S',1,1,2,4)
+        zbc('S',1,0,0,2)
+        gate(0,1)
+        gate(0,3)
+        zbc('V',1,0,2,4)
+        gate(0,0)
+        ld_v(0,1,0,4)
+        ld_v(1,1,0,4)
+        addv(0,1,3)
+        mz(1,1,1)
+        mz(0,1,0)
+        mz(1,1,3)
+        ml(1,0)
+        ramp('G',1,0)
+        gate(1,0)
+        zbc('S',0,1,0,2)
+        addv(1,1,1)
+        addv(1,1,3)
+        dist(1,1,3)
+        mz(1,1,2)
+        mz(1,1,0)
+        addv(1,1,0)
+        dist(1,1,0)
+        ml(1,1)
+        ramp('G',1,3)
+        mz(0,1,1)
+        mz(0,1,2)
+        addv(1,1,2)
+        addv(0,1,2)
+        addv(0,1,0)
+        ml(1,3)
+        ml(0,2)
+        ramp('G',0,2)
+        ramp('G',1,2)
+        zbc('S',1,1,0,2)
+        dq(0,0,1)
+        dist(1,1,1)
+        dq(1,0,1)
+        addv(0,1,1)
+        zbq(0,0)
+        dq(0,1,2)
+        dist(0,1,1)
+        dist(0,1,2)
+        dist(0,1,3)
+        ml(1,2)
+        ramp('G',1,1)
+        gate(1,1)
+        zbq(1,0)
+        dq(0,3,4)
+        mo(0,0)
+        zbq(0,1)
+        dq(1,1,2)
+        zbq(1,1)
+        ml(0,5)
+        dist(0,1,0)
+        mo(1,1)
+        dist(1,1,2)
+        mo(1,0)
+        gate(1,3)
+        oround('S',0,0)
+        ocopy('S',0,0)
+        gate(1,2)
+        ramp('G',0,5)
+        ramp('G',1,4)
+        ramp('S',1,5)
+        ml(1,5)
+        gate(0,2)
+        ml(1,4)
+        dq(1,2,3)
+        dq(1,3,4)
+        dq(0,2,3)
+        ocopy('S',1,0)
+        oround('S',1,0)
+        ocopy('S',1,1)
+        mo(0,1)
+        ramp('S',0,6)
+        gate(1,5)
+        gate(0,5)
+        gate(1,4)
+        ml(0,4)
+        mo(0,3)
+        mo(1,2)
+        ocopy('V',0,1)
+        ramp('G',0,4)
+        st_f('Y',1,0,2)
+        ramp('G',1,7)
+        gate(0,4)
+        oround('V',0,1)
+        dq(1,4,5)
+        dq(1,5,6)
+        ocopy('S',0,3)
+        oq(0,1,2)
+        oq(1,0,1)
+        dq(0,4,5)
+        mo(0,2)
+        ocopy('S',1,2)
+        mo(1,3)
+        dq(0,5,6)
+        oround('V',1,1)
+        ocopy('S',0,2)
+        ml(1,6)
+        ramp('G',1,6)
+        oround('S',1,3)
+        ocopy('S',1,3)
+        oround('S',1,2)
+        oround('S',0,2)
+        ml(0,7)
+        ml(0,6)
+        oq(0,0,1)
+        mo(1,4)
+        ocopy('S',1,4)
+        st_f('Y',0,0,2)
+        mo(1,5)
+        ocopy('S',1,5)
+        ml(1,7)
+        mo(0,4)
+        st_f('Y',0,2,4)
+        st_f('Y',1,2,4)
+        gate(0,6)
+        gate(1,6)
+        ocopy('S',0,4)
+        oq(1,1,2)
+        st_c('Y',0,2)
+        st_f('Y',1,4,6)
+        dq(0,6,7)
+        dq(1,6,7)
+        mo(1,6)
+        ramp('G',0,7)
+        oround('V',0,3)
+        ocopy('S',1,6)
+        st_f('Y',1,6,7)
+        gate(0,7)
+        oq(1,2,3)
+        mo(0,5)
+        ocopy('S',0,5)
+        gate(1,7)
+        st_f('Y',0,4,6)
+        oround('S',1,4)
+        dq(0,7,8)
+        oq(1,3,4)
+        dq(1,7,8)
+        oq(0,2,3)
+        mo(0,6)
+        ocopy('V',0,6)
+        oq(0,3,4)
+        oround('V',0,4)
+        oround('V',0,5)
+        oround('V',0,6)
+        st_f('Y',0,6,7)
+        st_c('Y',2,4)
+        oq(0,4,5)
+        oround('S',1,6)
+        oq(1,6,7)
+        oq(1,4,5)
+        oround('S',1,5)
+        oq(1,5,6)
+        mo(1,7)
+        oq(0,5,6)
+        ocopy('S',1,7)
+        st_f('Y',1,7,8)
+        mo(0,7)
+        ocopy('S',0,7)
+        oround('V',0,7)
+        st_f('Y',0,7,8)
+        st_c('Y',4,6)
+        oround('S',1,7)
+        oq(1,7,8)
+        oq(0,6,7)
+        oq(0,7,8)
+        st_s('S',3)
+        st_s('Y',2)
+        st_c('Y',6,8)
+        st_s('Y',0)
+        st_s('S',1)

@@ -17,6 +17,9 @@ ALU = mybir.AluOpType
 ACT = mybir.ActivationFunctionType
 
 P = 128
+H = 512
+RUN = 2
+ZG = 2
 
 
 def tile_epropeligibilityweightupdate_x2_kernel(
@@ -25,43 +28,35 @@ def tile_epropeligibilityweightupdate_x2_kernel(
     nc = tc.nc
     with ExitStack() as ctx:
         keep = ctx.enter_context(tc.tile_pool(name="keep", bufs=1))
-        stage = ctx.enter_context(tc.tile_pool(name="stage", bufs=1))
-        wide = ctx.enter_context(tc.tile_pool(name="wide", bufs=4))
         psum = ctx.enter_context(tc.psum_pool(name="psum", bufs=1))
         ctx.enter_context(tc.manual_schedule())
 
-        ident = keep.tile([P, P], F32, name="ident")
-        z_sb = keep.tile([P, 2, 4, PRE], BF16, name="z_sb", align_bytes=64)
-        e_sb = keep.tile([P, 2, 4, O], BF16, name="e_sb", align_bytes=64)
-        v_sb = keep.tile([P, 2, 4, N], BF16, name="v_sb", align_bytes=64)
-        zb_sb = keep.tile([P, 2, 4, PRE], BF16, name="zb_sb", align_bytes=64)
-        w_words = keep.tile([P, 2, 2 * N], U8, name="w_words", align_bytes=64)
-        b_words = keep.tile([P, 2 * N], U8, name="b_words", align_bytes=64)
-        w_scales = keep.tile([P, 2, N], U8, name="w_scales", align_bytes=64)
-        b_scales = keep.tile([P, N], U8, name="b_scales", align_bytes=64)
-        z_codes = keep.tile([P, 2, 4, 2 * P], U32, name="z_codes", align_bytes=64)
-        z_scales = keep.tile([P, 2, 4, 2 * P], U8, name="z_scales", align_bytes=64)
-        e_codes = keep.tile([P, 2, 4 * P], U32, name="e_codes", align_bytes=64)
-        e_scales = keep.tile([P, 2, 4 * P], U8, name="e_scales", align_bytes=64)
-        zb_codes = keep.tile([P, 2, PRE], U32, name="zb_codes", align_bytes=64)
-        zb_scales = keep.tile([P, 2, PRE], U8, name="zb_scales", align_bytes=64)
-        d_codes = keep.tile([P, 2, N], U32, name="d_codes", align_bytes=64)
-        d_scales = keep.tile([P, 2, N], U8, name="d_scales", align_bytes=64)
-        o_f32 = keep.tile([P, 2, 4, N], F32, name="o_f32", align_bytes=64)
-        o_codes = keep.tile([P, 2, N], U32, name="o_codes", align_bytes=64)
-        o_scales = keep.tile([P, 2, N], U8, name="o_scales", align_bytes=64)
-        warm = keep.tile([P, 16], F32, name="warm")
+        def tile(name, shape, dtype):
+            return keep.tile(shape, dtype, name=name, align_bytes=64)
 
-        def rows(x, g):
-            return x[512 * g : 512 * (g + 1), :].rearrange("(p t) c -> p t c", t=4)
-
-        def copy(eng, out, in_):
-            if eng == "S":
-                nc.scalar.copy(out=out, in_=in_)
-            elif eng == "V":
-                nc.vector.tensor_copy(out=out, in_=in_)
-            else:
-                nc.gpsimd.tensor_scalar(out=out, in0=in_, scalar1=1.0, scalar2=0.0, op0=ALU.mult, op1=ALU.add)
+        both = range(2)
+        ident = tile("ident", [P, P], F32)
+        z_sb = {(g, j): tile("z%d%d" % (g, j), [P, 2 * PRE], BF16) for g in both for j in both}
+        e_sb = {g: tile("e%d" % g, [P, 4 * O], BF16) for g in both}
+        v_sb = {(g, h): tile("v%d%d" % (g, h), [P, 4, H], BF16) for g in both for h in both}
+        zb_sb = {(g, i): tile("zb%d%d" % (g, i), [P, 4, H], BF16) for g in both for i in both}
+        w_words = {h: tile("w%d" % h, [P, 2, 2 * H], U8) for h in both}
+        b_words = tile("b_words", [P, 2 * N], U8)
+        w_scales = tile("w_scales", [P, 2, N], U8)
+        b_scales = tile("b_scales", [P, N], U8)
+        z_codes = {(g, j): tile("zc%d%d" % (g, j), [P, 4 * P], U32) for g in both for j in both}
+        z_scales = {(g, j): tile("zs%d%d" % (g, j), [P, 4 * P], U8) for g in both for j in both}
+        e_codes = {g: tile("ec%d" % g, [P, 4 * P], U32) for g in both}
+        e_scales = {g: tile("es%d" % g, [P, 4 * P], U8) for g in both}
+        zb_codes = {(g, i): tile("zbc%d%d" % (g, i), [P, H], U32) for g in both for i in both}
+        zb_scales = {(g, i): tile("zbs%d%d" % (g, i), [P, H], U8) for g in both for i in both}
+        d_codes = {(g, h): tile("dc%d%d" % (g, h), [P, H], U32) for g in both for h in both}
+        d_scales = {(g, h): tile("ds%d%d" % (g, h), [P, H], U8) for g in both for h in both}
+        o_f32 = {(i, h): tile("of%d%d" % (i, h), [P, 4, H], F32) for i in both for h in both}
+        o_codes = {h: tile("oc%d" % h, [P, 2, H], U32) for h in both}
+        o_scales = {h: tile("os%d" % h, [P, 2, H], U8) for h in both}
+        junk = tile("junk", [P, H], BF16)
+        warm = tile("warm", [P, 16], F32)
 
         live = {}
         count = {}
@@ -71,459 +66,361 @@ def tile_epropeligibilityweightupdate_x2_kernel(
             count[name] = n + 1
             return pool.tile(shape, dtype, name="%s%d" % (name, n % depth), **kw)
 
-        def setup():
-            nc.vector.memset(w_scales[:].rearrange("p c n -> p (c n)").bitcast(I32), 0)
-            nc.vector.memset(b_scales[:].bitcast(I32), 0)
-            nc.vector.memset(warm[:, 0:1], 0.0)
-            nc.scalar.activation(out=warm[:, 8:9], in_=warm[:, 0:1], func=ACT.Abs)
+        def staged(key, depth, shape, dtype):
+            if key not in live:
+                live[key] = ring(keep, key[0], depth, shape, dtype, align_bytes=64)
+            return live[key]
 
-        def mkident():
-            make_identity(nc, ident[:])
+        def bank():
+            return ring(psum, "bank", 8, [P, H], F32)
+
+        def rows(x, g):
+            return x[512 * g : 512 * (g + 1), :].rearrange("(p t) c -> p t c", t=4)
+
+        def half(h):
+            return slice(H * h, H * (h + 1))
+
+        def copy(eng, out, in_):
+            if eng == "S":
+                nc.scalar.copy(out=out, in_=in_)
+            elif eng == "V":
+                nc.vector.tensor_copy(out=out, in_=in_)
+            else:
+                nc.gpsimd.tensor_scalar(out=out, in0=in_, scalar1=1.0, scalar2=0.0, op0=ALU.mult, op1=ALU.add)
 
         def queue(eng):
             return {"S": nc.scalar, "G": nc.gpsimd, "Y": nc.sync}[eng]
 
-        def ld_z(g, t0, t1):
-            nc.sync.dma_start(out=z_sb[:, g, t0:t1, :], in_=rows(z, g)[:, t0:t1, :])
+        def setup():
+            nc.vector.memset(w_scales[:].rearrange("p c n -> p (c n)").bitcast(I32), 0)
+            nc.vector.memset(b_scales[:].bitcast(I32), 0)
+            make_identity(nc, ident[:])
+
+        def warmact():
+            nc.vector.memset(warm[:, 0:1], 0.0)
+            nc.scalar.activation(out=warm[:, 8:9], in_=warm[:, 0:1], func=ACT.Abs)
+
+        def warmpe(n):
+            b = bank()
+            for k in range(n):
+                nc.tensor.matmul(b[:], lhsT=junk[:, 0:P], rhs=junk[:], start=True, stop=True)
+
+        def ld_z(g, j, a0=0, a1=2):
+            src = rows(z, g)[:, 2 * j + a0 : 2 * j + a1, :].rearrange("p t c -> p (t c)")
+            nc.sync.dma_start(out=z_sb[g, j][:, PRE * a0 : PRE * a1], in_=src)
 
         def ld_e(g):
-            nc.sync.dma_start(out=e_sb[:, g, :, :], in_=rows(err, g))
+            nc.sync.dma_start(out=e_sb[g][:], in_=rows(err, g).rearrange("p t c -> p (t c)"))
 
-        def ld_v(g, h, t0, t1):
-            nc.sync.dma_start(out=v_sb[:, g, t0:t1, 512 * h : 512 * (h + 1)], in_=rows(v0, g)[:, t0:t1, 512 * h : 512 * (h + 1)])
+        def ld_v(g, h, t0=0, t1=4):
+            nc.sync.dma_start(out=v_sb[g, h][:, t0:t1, :], in_=rows(v0, g)[:, t0:t1, half(h)])
 
-        def ld_zb(g):
-            nc.sync.dma_start(out=zb_sb[:, g, :, :], in_=rows(zbar, g))
+        def ld_zb(g, i):
+            nc.sync.dma_start(out=zb_sb[g, i][:], in_=rows(zbar, g)[:, :, half(i)])
 
         def ld_w(h):
-            b = slice(N * h, N * (h + 1))
-            nc.sync.dma_start(out=w_words[:, :, b].bitcast(I32), in_=wrec_words.rearrange("c p b -> p c b")[:, :, b].bitcast(I32))
+            src = wrec_words.rearrange("c p b -> p c b")[:, :, 2 * H * h : 2 * H * (h + 1)]
+            nc.sync.dma_start(out=w_words[h][:].bitcast(I32), in_=src.bitcast(I32))
 
         def ld_b():
             nc.sync.dma_start(out=b_words[:].bitcast(I32), in_=bfb_words[0].bitcast(I32))
 
-        def ld_ws(eng, q):
-            if True:
+        def ld_ws(eng):
+            for q in range(4):
                 queue(eng).dma_start(
                     out=w_scales[32 * q : 32 * q + 4, :, :].bitcast(I32),
                     in_=wrec_scales[:, 4 * q : 4 * q + 4, :].rearrange("c r n -> r c n").bitcast(I32),
                 )
 
-        def ld_bs(eng, q):
-            if True:
+        def ld_bs(eng):
+            for q in range(4):
                 queue(eng).dma_start(
                     out=b_scales[32 * q : 32 * q + 4, :].bitcast(I32),
                     in_=bfb_scales[0, 4 * q : 4 * q + 4, :].bitcast(I32),
                 )
 
-        def turn(key, sources):
-            bank = ring(psum, "bank", 8, [P, 512], F32)
-            for a, words in enumerate(sources):
-                for u in range(2):
-                    j = 2 * a + u
-                    nc.tensor.transpose(bank[:, P * j : P * (j + 1)], words[:, u : 2 * P : 2], ident[:])
-            live[key] = bank
-
-        def tz(g, t):
-            words = z_sb[:, g, t, :].bitcast(F32)
-            turn(("z", g, t), [words[:, 256 * c : 256 * (c + 1)] for c in range(2)])
-
-        def te(g, j):
-            turn(("e", g, j), [e_sb[:, g, 2 * j + a, :].bitcast(F32) for a in range(2)])
+        def turn(kind, g, j):
+            if kind == "z":
+                words = z_sb[g, j // 2][:, PRE * (j % 2) : PRE * (j % 2 + 1)].bitcast(F32)
+            else:
+                words = e_sb[g][:, 2 * O * j : 2 * O * (j + 1)].bitcast(F32)
+            b = bank()
+            for a in both:
+                for u in both:
+                    k = 2 * a + u
+                    nc.tensor.transpose(b[:, P * k : P * (k + 1)], words[:, 2 * P * a + u : 2 * P * (a + 1) : 2], ident[:])
+            live["bank", kind, g, j] = b
 
         def tcopy(eng, kind, g, j):
-            bank = live.pop((kind, g, j))
-            turned = ring(stage, "turned", 6, [P, 1024], BF16, align_bytes=64)
-            copy(eng, turned[:].bitcast(F32).rearrange("p (a m u) -> p a m u", a=2, u=2),
-                 bank[:].rearrange("p (a u m) -> p a m u", a=2, u=2))
-            live[("t", kind, g, j)] = turned
+            turned = staged(("turned", kind, g, j // 2), 3, [P, 2048], BF16)
+            dst = turned[:, 1024 * (j % 2) : 1024 * (j % 2 + 1)].bitcast(F32)
+            copy(eng, dst.rearrange("p (a m u) -> p a m u", a=2, u=2),
+                 live.pop(("bank", kind, g, j))[:].rearrange("p (a u m) -> p a m u", a=2, u=2))
 
-        def tq(kind, g, j):
-            turned = live.pop(("t", kind, g, j))
-            if kind == "z":
-                codes, scales = z_codes[:, g, j, :], z_scales[:, g, j, :]
-            else:
-                codes, scales = e_codes[:, g, 256 * j : 256 * (j + 1)], e_scales[:, g, 256 * j : 256 * (j + 1)]
-            nc.vector.quantize_mx(out=codes.bitcast(FP8X4), scales=scales, in_=turned[:])
+        def tq(kind, g, j, a0=0, a1=2):
+            codes, scales = (z_codes[g, j], z_scales[g, j]) if kind == "z" else (e_codes[g], e_scales[g])
+            c = slice(256 * a0, 256 * a1)
+            nc.vector.quantize_mx(out=codes[:, c].bitcast(FP8X4), scales=scales[:, c],
+                                  in_=live["turned", kind, g, j][:, 1024 * a0 : 1024 * a1])
 
         def mz(g, h, t):
-            bank = ring(psum, "bank", 8, [P, 512], F32)
-            for c in range(2):
+            b = bank()
+            for c in both:
+                col = slice(P * (2 * (t % 2) + c), P * (2 * (t % 2) + c + 1))
                 nc.tensor.matmul_mx(
-                    out=bank[:],
-                    lhsT=z_codes[:, g, t, P * c : P * (c + 1)].bitcast(FP8X4),
-                    lhsT_scale=z_scales[:, g, t, P * c : P * (c + 1)],
-                    rhs=w_words[:, c, N * h : N * (h + 1)].bitcast(FP4X4),
-                    rhs_scale=w_scales[:, c, 512 * h : 512 * (h + 1)],
+                    out=b[:],
+                    lhsT=z_codes[g, t // 2][:, col].bitcast(FP8X4), lhsT_scale=z_scales[g, t // 2][:, col],
+                    rhs=w_words[h][:, c, :].bitcast(FP4X4), rhs_scale=w_scales[:, c, half(h)],
                     start=(c == 0), stop=(c == 1))
-            live[("zw", g, h, t)] = bank
+            live["zw", g, h, t] = b
 
         def addv(g, h, t):
-            bank = live.pop(("zw", g, h, t))
-            if ("v", g, h) not in live:
-                live[("v", g, h)] = wide.tile([P, 4, 512], F32, name="v_f32", align_bytes=64)
+            v = staged(("psi", g, h), 4, [P, 4, H], F32)
             nc.vector.scalar_tensor_tensor(
-                out=live[("v", g, h)][:, t, :], in0=v_sb[:, g, t, 512 * h : 512 * (h + 1)], scalar=0.8,
-                in1=bank[:], op0=ALU.mult, op1=ALU.add)
+                out=v[:, t, :], in0=v_sb[g, h][:, t, :], scalar=0.8,
+                in1=live.pop(("zw", g, h, t))[:], op0=ALU.mult, op1=ALU.add)
 
-        def dist(g, h, t):
-            nc.scalar.activation(out=live[("v", g, h)][:, t, :], in_=live[("v", g, h)][:, t, :], func=ACT.Abs, bias=-1.0, scale=1.0)
+        def dist(g, h, t0, t1, c0=0, c1=H):
+            v = live["psi", g, h][:, t0:t1, c0:c1]
+            nc.scalar.activation(out=v, in_=v, func=ACT.Abs, bias=-1.0, scale=1.0)
 
-        def ramp(eng, g, q):
-            src = live[("v", g, q // 4)][:, :, P * (q % 4) : P * (q % 4 + 1)].rearrange("p t n -> p n t")
-            w = ring(stage, "ramp", 6, [P, P, 4], F32, align_bytes=64)
-            if eng == "S":
-                nc.scalar.activation(out=w[:], in_=src, func=ACT.Identity, bias=0.3, scale=-0.3)
-            else:
-                (nc.vector if eng == "V" else nc.gpsimd).tensor_scalar(
-                    out=w[:], in0=src, scalar1=-0.3, scalar2=0.3, op0=ALU.mult, op1=ALU.add)
-            live[("w", g, q)] = w
+        def ramp(g, h, t0, t1, c0=0, c1=H):
+            v = live["psi", g, h][:, t0:t1, c0:c1]
+            nc.scalar.activation(out=v, in_=v, func=ACT.Relu, bias=0.3, scale=-0.3)
 
-        def ml(g, q):
-            bank = ring(psum, "bank", 8, [P, 512], F32)
+        def ml(g, h, q):
+            b = bank()
+            n0 = H * h + P * q
             for t in range(4):
                 nc.tensor.matmul_mx(
-                    out=bank[:, P * t : P * (t + 1)],
-                    lhsT=e_codes[:, g, P * t : P * (t + 1)].bitcast(FP8X4),
-                    lhsT_scale=e_scales[:, g, P * t : P * (t + 1)],
-                    rhs=b_words[:, 2 * P * q : 2 * P * (q + 1)].bitcast(FP4X4),
-                    rhs_scale=b_scales[:, P * q : P * (q + 1)],
+                    out=b[:, P * t : P * (t + 1)],
+                    lhsT=e_codes[g][:, P * t : P * (t + 1)].bitcast(FP8X4), lhsT_scale=e_scales[g][:, P * t : P * (t + 1)],
+                    rhs=b_words[:, 2 * n0 : 2 * (n0 + P)].bitcast(FP4X4), rhs_scale=b_scales[:, n0 : n0 + P],
                     start=True, stop=True)
-            live[("l", g, q)] = bank
+            live["l", g, h, q] = b
 
-        def gate(g, q):
-            bank = live.pop(("l", g, q))
-            d = ring(stage, "d_bf", 8, [P, P, 4], BF16, align_bytes=64)
-            nc.vector.scalar_tensor_tensor(
-                out=d[:], in0=live.pop(("w", g, q))[:], scalar=0.0,
-                in1=bank[:].rearrange("p (t n) -> p n t", t=4), op0=ALU.max, op1=ALU.mult)
-            live[("d", g, q)] = d
+        def gate(g, h, q):
+            d = staged(("d", g, h), 3, [P, H, 4], BF16)
+            cols = slice(P * q, P * (q + 1))
+            nc.vector.tensor_tensor(
+                out=d[:, cols, :].rearrange("p (c i) t -> p c t i", i=RUN),
+                in0=live["psi", g, h][:, :, cols].rearrange("p t (c i) -> p c t i", i=RUN),
+                in1=live.pop(("l", g, h, q))[:].rearrange("p (t c i) -> p c t i", t=4, i=RUN),
+                op=ALU.mult)
 
-        def dq(g, q, q1):
+        def dq(g, h, c0=0, c1=H):
             nc.vector.quantize_mx(
-                out=d_codes[:, g, P * q : P * (q + 1)].bitcast(FP8X4), scales=d_scales[:, g, P * q : P * (q + 1)],
-                in_=live.pop(("d", g, q))[:].rearrange("p n t -> p (n t)"))
+                out=d_codes[g, h][:, c0:c1].bitcast(FP8X4), scales=d_scales[g, h][:, c0:c1],
+                in_=live["d", g, h][:, c0:c1, :].rearrange("p n t -> p (n t)"))
 
-        def zbc(eng, g, i, s0, s1):
-            if ("zb", g, i) not in live:
-                live[("zb", g, i)] = wide.tile([P, 4, P, 4], BF16, name="zb_grouped", align_bytes=64)
-            copy(eng, live[("zb", g, i)][:, s0:s1, :, :],
-                 zb_sb[:, g, :, 512 * i : 512 * (i + 1)].rearrange("p t (m s) -> p s m t", s=4)[:, s0:s1, :, :])
+        def zc(eng, g, i, m0=0, m1=P):
+            grouped = staged(("zg", g, i), ZG, [P, 4, P, 4], BF16)
+            copy(eng, grouped[:, :, m0:m1, :].rearrange("p s m t -> p m s t"),
+                 zb_sb[g, i][:].rearrange("p t (m s) -> p m s t", s=4)[:, m0:m1, :, :])
 
-        def zbq(g, i):
+        def zq(g, i):
             nc.vector.quantize_mx(
-                out=zb_codes[:, g, 512 * i : 512 * (i + 1)].bitcast(FP8X4), scales=zb_scales[:, g, 512 * i : 512 * (i + 1)],
-                in_=live.pop(("zb", g, i))[:].rearrange("p s m t -> p (s m t)"))
+                out=zb_codes[g, i][:].bitcast(FP8X4), scales=zb_scales[g, i][:],
+                in_=live["zg", g, i][:].rearrange("p s m t -> p (s m t)"))
 
-        def mo(i, q):
-            bank = ring(psum, "bank", 8, [P, 512], F32)
-            for s in range(4):
-                c = slice(512 * i + P * s, 512 * i + P * (s + 1))
-                for g in range(2):
+        def mo(i, h, c0, width, k):
+            b = bank()
+            per = H // width
+            c = slice(c0, c0 + width)
+            for a in range(per):
+                s = per * k + a
+                for g in both:
                     nc.tensor.matmul_mx(
-                        out=bank[:, P * s : P * (s + 1)],
-                        lhsT=zb_codes[:, g, c].bitcast(FP8X4), lhsT_scale=zb_scales[:, g, c],
-                        rhs=d_codes[:, g, P * q : P * (q + 1)].bitcast(FP8X4), rhs_scale=d_scales[:, g, P * q : P * (q + 1)],
+                        out=b[:, width * a : width * (a + 1)],
+                        lhsT=zb_codes[g, i][:, P * s : P * (s + 1)].bitcast(FP8X4), lhsT_scale=zb_scales[g, i][:, P * s : P * (s + 1)],
+                        rhs=d_codes[g, h][:, c].bitcast(FP8X4), rhs_scale=d_scales[g, h][:, c],
                         start=(g == 0), stop=(g == 1))
-            live[("o", i, q)] = bank
+            live["o", i, h, c0, k] = b
 
-        def ocopy(eng, i, q):
-            copy(eng, o_f32[:, i, :, P * q : P * (q + 1)], live[("o", i, q)][:].rearrange("p (s n) -> p s n", s=4))
+        def ocopy(eng, i, h, c0, width, k):
+            per = H // width
+            copy(eng, o_f32[i, h][:, per * k : per * (k + 1), c0 : c0 + width],
+                 live.pop(("o", i, h, c0, k))[:].rearrange("p (a n) -> p a n", a=per))
 
-        def oround(eng, i, q):
-            ob = ring(stage, "o_bf", 8, [P, P, 4], BF16, align_bytes=64)
-            if eng != "V":
-                copy("S" if eng == "S" else "V", ob[:], live[("o", i, q)][:].rearrange("p (s n) -> p n s", s=4))
-            else:
-                copy(eng, ob[:], o_f32[:, i, :, P * q : P * (q + 1)].rearrange("p s n -> p n s"))
-            live[("ob", i, q)] = ob
+        def oround(eng, i, h, c0, c1):
+            ob = staged(("ob", i, h), 2, [P, H, 4], BF16)
+            copy(eng, ob[:, c0:c1, :].rearrange("p (c i) s -> p c s i", i=4),
+                 o_f32[i, h][:, :, c0:c1].rearrange("p s (c i) -> p c s i", i=4))
 
-        def oq(i, q, q1):
+        def oq(i, h, c0, c1):
             nc.vector.quantize_mx(
-                out=o_codes[:, i, P * q : P * (q + 1)].bitcast(FP8X4), scales=o_scales[:, i, P * q : P * (q + 1)],
-                in_=live.pop(("ob", i, q))[:].rearrange("p n s -> p (n s)"))
+                out=o_codes[h][:, i, c0:c1].bitcast(FP8X4), scales=o_scales[h][:, i, c0:c1],
+                in_=live["ob", i, h][:, c0:c1, :].rearrange("p n s -> p (n s)"))
 
-        def st_f(eng, i, q0, q1):
-            c = slice(P * q0, P * q1)
-            queue(eng).dma_start(out=rows(out_0, i)[:, :, c], in_=o_f32[:, i, :, c])
+        def st_f(eng, i, h, c0, c1, s0=0, s1=4):
+            queue(eng).dma_start(out=rows(out_0, i)[:, s0:s1, H * h + c0 : H * h + c1], in_=o_f32[i, h][:, s0:s1, c0:c1])
 
-        def st_c(eng, q0, q1):
-            c = slice(P * q0, P * q1)
+        def st_c(eng, i, h, c0, c1):
+            dst = out_1[i].rearrange("p m t -> p (m t)").bitcast(I32)[:, H * h + c0 : H * h + c1]
+            queue(eng).dma_start(out=dst, in_=o_codes[h][:, i, c0:c1].bitcast(I32))
+
+        def st_s(eng, h, q):
             queue(eng).dma_start(
-                out=out_1.rearrange("g p m t -> p g (m t)").bitcast(I32)[:, :, c], in_=o_codes[:, :, c].bitcast(I32))
+                out=out_2[:, 4 * q : 4 * q + 4, half(h)].rearrange("g r n -> r g n").bitcast(I32),
+                in_=o_scales[h][32 * q : 32 * q + 4, :, :].bitcast(I32))
 
-        def st_s(eng, q):
-            queue(eng).dma_start(
-                out=out_2[:, 4 * q : 4 * q + 4, :].rearrange("g r n -> r g n").bitcast(I32),
-                in_=o_scales[32 * q : 32 * q + 4, :, :].bitcast(I32))
-
+        ld_z(0, 0, 0, 1)
+        ld_z(0, 0, 1, 2)
         setup()
-        mkident()
-        ld_z(0,0,1)
-        tz(0,0)
-        tcopy('V','z',0,0)
-        tq('z',0,0)
-        ld_z(0,1,2)
-        tz(0,1)
-        ld_z(0,3,4)
-        ld_ws('S',2)
-        tz(0,3)
-        ld_ws('S',3)
-        tcopy('V','z',0,1)
-        ld_ws('S',1)
-        ld_bs('G',3)
-        ld_ws('S',0)
-        ld_z(0,2,3)
-        tcopy('S','z',0,3)
-        tz(0,2)
+        ld_ws("S")
+        ld_z(0, 1)
         ld_w(0)
-        tq('z',0,1)
-        tq('z',0,3)
-        tcopy('V','z',0,2)
-        tq('z',0,2)
-        ld_v(0,0,0,2)
-        mz(0,0,0)
-        addv(0,0,0)
-        dist(0,0,0)
-        mz(0,0,1)
-        addv(0,0,1)
-        mz(0,0,3)
-        ld_bs('G',1)
-        mz(0,0,2)
-        ld_v(0,0,2,4)
+        ld_v(0, 0, 0, 2)
+        ld_v(0, 0, 2, 4)
         ld_e(0)
-        te(0,0)
-        addv(0,0,2)
-        ld_z(1,2,4)
-        ld_e(1)
-        tz(1,2)
-        addv(0,0,3)
-        tcopy('V','z',1,2)
-        dist(0,0,1)
-        te(0,1)
-        ld_z(1,0,2)
-        tcopy('V','e',0,1)
-        tq('z',1,2)
-        dist(0,0,2)
-        tcopy('S','e',0,0)
-        tq('e',0,1)
-        tz(1,3)
-        te(1,1)
-        tcopy('V','e',1,1)
-        tq('e',0,0)
-        tcopy('S','z',1,3)
-        te(1,0)
-        dist(0,0,3)
-        tq('z',1,3)
-        ramp('V',0,3)
-        ld_bs('G',0)
-        ld_bs('G',2)
-        ramp('G',0,0)
-        tcopy('S','e',1,0)
-        tq('e',1,0)
-        tq('e',1,1)
-        ramp('G',0,1)
-        tz(1,0)
-        tcopy('S','z',1,0)
-        tq('z',1,0)
-        tz(1,1)
-        tcopy('S','z',1,1)
-        tq('z',1,1)
-        ld_zb(0)
-        zbc('S',0,1,2,4)
-        zbc('S',0,0,0,2)
-        zbc('V',0,0,2,4)
-        ld_v(1,0,0,4)
-        mz(1,0,3)
-        addv(1,0,3)
-        mz(1,0,0)
-        addv(1,0,0)
-        dist(1,0,0)
-        dist(1,0,3)
-        mz(1,0,2)
-        mz(1,0,1)
-        addv(1,0,2)
-        dist(1,0,2)
+        ld_bs("Y")
+        ld_z(1, 0)
+        ld_zb(0, 0)
         ld_b()
+        ld_z(1, 1)
+        ld_e(1)
+        ld_v(1, 0)
+        ld_zb(1, 0)
         ld_w(1)
-        ml(0,1)
-        ml(0,3)
-        ml(0,0)
-        mz(0,1,3)
-        addv(1,0,1)
-        dist(1,0,1)
-        ld_zb(1)
-        zbc('S',1,1,2,4)
-        zbc('S',1,0,0,2)
-        gate(0,1)
-        gate(0,3)
-        zbc('V',1,0,2,4)
-        gate(0,0)
-        ld_v(0,1,0,4)
-        ld_v(1,1,0,4)
-        addv(0,1,3)
-        mz(1,1,1)
-        mz(0,1,0)
-        mz(1,1,3)
-        ml(1,0)
-        ramp('G',1,0)
-        gate(1,0)
-        zbc('S',0,1,0,2)
-        addv(1,1,1)
-        addv(1,1,3)
-        dist(1,1,3)
-        mz(1,1,2)
-        mz(1,1,0)
-        addv(1,1,0)
-        dist(1,1,0)
-        ml(1,1)
-        ramp('G',1,3)
-        mz(0,1,1)
-        mz(0,1,2)
-        addv(1,1,2)
-        addv(0,1,2)
-        addv(0,1,0)
-        ml(1,3)
-        ml(0,2)
-        ramp('G',0,2)
-        ramp('G',1,2)
-        zbc('S',1,1,0,2)
-        dq(0,0,1)
-        dist(1,1,1)
-        dq(1,0,1)
-        addv(0,1,1)
-        zbq(0,0)
-        dq(0,1,2)
-        dist(0,1,1)
-        dist(0,1,2)
-        dist(0,1,3)
-        ml(1,2)
-        ramp('G',1,1)
-        gate(1,1)
-        zbq(1,0)
-        dq(0,3,4)
-        mo(0,0)
-        zbq(0,1)
-        dq(1,1,2)
-        zbq(1,1)
-        ml(0,5)
-        dist(0,1,0)
-        mo(1,1)
-        dist(1,1,2)
-        mo(1,0)
-        gate(1,3)
-        oround('S',0,0)
-        ocopy('S',0,0)
-        gate(1,2)
-        ramp('G',0,5)
-        ramp('G',1,4)
-        ramp('S',1,5)
-        ml(1,5)
-        gate(0,2)
-        ml(1,4)
-        dq(1,2,3)
-        dq(1,3,4)
-        dq(0,2,3)
-        ocopy('S',1,0)
-        oround('S',1,0)
-        ocopy('S',1,1)
-        mo(0,1)
-        ramp('S',0,6)
-        gate(1,5)
-        gate(0,5)
-        gate(1,4)
-        ml(0,4)
-        mo(0,3)
-        mo(1,2)
-        ocopy('V',0,1)
-        ramp('G',0,4)
-        st_f('Y',1,0,2)
-        ramp('G',1,7)
-        gate(0,4)
-        oround('V',0,1)
-        dq(1,4,5)
-        dq(1,5,6)
-        ocopy('S',0,3)
-        oq(0,1,2)
-        oq(1,0,1)
-        dq(0,4,5)
-        mo(0,2)
-        ocopy('S',1,2)
-        mo(1,3)
-        dq(0,5,6)
-        oround('V',1,1)
-        ocopy('S',0,2)
-        ml(1,6)
-        ramp('G',1,6)
-        oround('S',1,3)
-        ocopy('S',1,3)
-        oround('S',1,2)
-        oround('S',0,2)
-        ml(0,7)
-        ml(0,6)
-        oq(0,0,1)
-        mo(1,4)
-        ocopy('S',1,4)
-        st_f('Y',0,0,2)
-        mo(1,5)
-        ocopy('S',1,5)
-        ml(1,7)
-        mo(0,4)
-        st_f('Y',0,2,4)
-        st_f('Y',1,2,4)
-        gate(0,6)
-        gate(1,6)
-        ocopy('S',0,4)
-        oq(1,1,2)
-        st_c('Y',0,2)
-        st_f('Y',1,4,6)
-        dq(0,6,7)
-        dq(1,6,7)
-        mo(1,6)
-        ramp('G',0,7)
-        oround('V',0,3)
-        ocopy('S',1,6)
-        st_f('Y',1,6,7)
-        gate(0,7)
-        oq(1,2,3)
-        mo(0,5)
-        ocopy('S',0,5)
-        gate(1,7)
-        st_f('Y',0,4,6)
-        oround('S',1,4)
-        dq(0,7,8)
-        oq(1,3,4)
-        dq(1,7,8)
-        oq(0,2,3)
-        mo(0,6)
-        ocopy('V',0,6)
-        oq(0,3,4)
-        oround('V',0,4)
-        oround('V',0,5)
-        oround('V',0,6)
-        st_f('Y',0,6,7)
-        st_c('Y',2,4)
-        oq(0,4,5)
-        oround('S',1,6)
-        oq(1,6,7)
-        oq(1,4,5)
-        oround('S',1,5)
-        oq(1,5,6)
-        mo(1,7)
-        oq(0,5,6)
-        ocopy('S',1,7)
-        st_f('Y',1,7,8)
-        mo(0,7)
-        ocopy('S',0,7)
-        oround('V',0,7)
-        st_f('Y',0,7,8)
-        st_c('Y',4,6)
-        oround('S',1,7)
-        oq(1,7,8)
-        oq(0,6,7)
-        oq(0,7,8)
-        st_s('S',3)
-        st_s('Y',2)
-        st_c('Y',6,8)
-        st_s('Y',0)
-        st_s('S',1)
+        ld_v(0, 1)
+        ld_zb(0, 1)
+        ld_v(1, 1)
+        ld_zb(1, 1)
+
+        warmact()
+        for t in range(4):
+            turn("z", 0, t)
+            tcopy("S", "z", 0, t)
+            if t < 2:
+                tq("z", 0, 0, t, t + 1)
+        tq("z", 0, 1)
+        for t in range(4):
+            mz(0, 0, t)
+        for j in both:
+            turn("e", 0, j)
+        for t in range(4):
+            addv(0, 0, t)
+            turn("z", 1, t)
+        dist(0, 0, 0, 2)
+        dist(0, 0, 2, 4)
+        for j in both:
+            tcopy("V", "e", 0, j)
+        for t in (0, 1):
+            tcopy("S", "z", 1, t)
+        zc("V", 0, 0)
+        tq("e", 0, 0)
+        ramp(0, 0, 0, 4, 0, 256)
+        ramp(0, 0, 0, 4, 256, 512)
+        tq("z", 1, 0)
+        zq(0, 0)
+        for q in range(4):
+            ml(0, 0, q)
+        for t in (2, 3):
+            tcopy("S", "z", 1, t)
+        for j in both:
+            turn("e", 1, j)
+        for t in (0, 1):
+            mz(1, 0, t)
+        for q in range(3):
+            gate(0, 0, q)
+        for j in both:
+            tcopy("S", "e", 1, j)
+        tq("z", 1, 1)
+        gate(0, 0, 3)
+        for t in (2, 3):
+            mz(1, 0, t)
+        zc("S", 1, 0)
+        for t in range(4):
+            addv(1, 0, t)
+            mz(0, 1, t)
+        tq("e", 1, 0)
+        dq(0, 0)
+        zq(1, 0)
+        for q in range(4):
+            ml(1, 0, q)
+        dist(1, 0, 0, 2)
+        dist(1, 0, 2, 4)
+        ramp(1, 0, 0, 4, 0, 256)
+        ramp(1, 0, 0, 4, 256, 512)
+        for t in range(4):
+            addv(0, 1, t)
+            mz(1, 1, t)
+        for q in range(4):
+            gate(1, 0, q)
+            ml(0, 1, q)
+        zc("S", 0, 1)
+        dist(0, 1, 0, 2)
+        dist(0, 1, 2, 4)
+        addv(1, 1, 0)
+        dq(1, 0)
+        zq(0, 1)
+        for t in range(1, 4):
+            addv(1, 1, t)
+        for s in range(4):
+            mo(0, 0, 0, 512, s)
+        zc("V", 1, 1)
+        ramp(0, 1, 0, 4, 0, 256)
+        for s in range(4):
+            ocopy("S", 0, 0, 0, 512, s)
+            if s % 2:
+                st_f("Y", 0, 0, 0, 512, s - 1, s + 1)
+        ramp(0, 1, 0, 4, 256, 512)
+        gate(0, 1, 0)
+        zq(1, 1)
+        gate(0, 1, 1)
+        for s in range(4):
+            mo(1, 0, 0, 512, s)
+        dist(1, 1, 0, 4, 0, 256)
+        oround("V", 0, 0, 0, 512)
+        for q in (2, 3):
+            gate(0, 1, q)
+        for q in range(4):
+            ml(1, 1, q)
+        ocopy("S", 1, 0, 0, 512, 0)
+        ramp(1, 1, 0, 4, 0, 256)
+        oq(0, 0, 0, 512)
+        st_c("Y", 0, 0, 0, 512)
+        dq(0, 1)
+        for s in range(1, 4):
+            ocopy("S", 1, 0, 0, 512, s)
+            if s % 2:
+                st_f("Y", 1, 0, 0, 512, s - 1, s + 1)
+        for q in (0, 1):
+            gate(1, 1, q)
+        dist(1, 1, 0, 4, 256, 512)
+        oround("V", 1, 0, 0, 512)
+        dq(1, 1, 0, 256)
+        oq(1, 0, 0, 512)
+        st_c("Y", 1, 0, 0, 512)
+        for i in both:
+            for k in both:
+                mo(i, 1, 0, 256, k)
+        ramp(1, 1, 0, 4, 256, 512)
+        for q in range(4):
+            st_s("Y", 0, q)
+        for q in (2, 3):
+            gate(1, 1, q)
+        for i in both:
+            for k in both:
+                ocopy("S", i, 1, 0, 256, k)
+            st_f("Y", i, 1, 0, 256)
+        oround("V", 0, 1, 0, 256)
+        dq(1, 1, 256, 512)
+        for i in both:
+            for k in both:
+                mo(i, 1, 256, 256, k)
+        oround("V", 1, 1, 0, 256)
+        for i in both:
+            oq(i, 1, 0, 256)
+            st_c("Y", i, 1, 0, 256)
+        for i in both:
+            for k in both:
+                ocopy("SV"[k], i, 1, 256, 256, k)
+            st_f("Y", i, 1, 256, 512)
+        for i in both:
+            oround("V", i, 1, 256, 512)
+        for i in both:
+            oq(i, 1, 256, 512)
+            st_c("Y", i, 1, 256, 512)
+        for q in range(4):
+            st_s("SY"[q % 2], 1, q)

@@ -18,8 +18,8 @@ ACT = mybir.ActivationFunctionType
 
 P = 128
 H = 512
-RUN = 2
-ZG = 2
+RUN = 4
+ZG = 1
 
 
 def tile_epropeligibilityweightupdate_x2_kernel(
@@ -38,8 +38,8 @@ def tile_epropeligibilityweightupdate_x2_kernel(
         ident = tile("ident", [P, P], F32)
         z_sb = {(g, j): tile("z%d%d" % (g, j), [P, 2 * PRE], BF16) for g in both for j in both}
         e_sb = {g: tile("e%d" % g, [P, 4 * O], BF16) for g in both}
-        v_sb = {(g, h): tile("v%d%d" % (g, h), [P, 4, H], BF16) for g in both for h in both}
-        zb_sb = {(g, i): tile("zb%d%d" % (g, i), [P, 4, H], BF16) for g in both for i in both}
+        v_sb = {(g, j): tile("v%d%d" % (g, j), [P, 2, N], BF16) for g in both for j in both}
+        zb_sb = {g: tile("zb%d" % g, [P, 4, PRE], BF16) for g in both}
         w_words = {h: tile("w%d" % h, [P, 2, 2 * H], U8) for h in both}
         b_words = tile("b_words", [P, 2 * N], U8)
         w_scales = tile("w_scales", [P, 2, N], U8)
@@ -55,7 +55,6 @@ def tile_epropeligibilityweightupdate_x2_kernel(
         o_f32 = {(i, h): tile("of%d%d" % (i, h), [P, 4, H], F32) for i in both for h in both}
         o_codes = {h: tile("oc%d" % h, [P, 2, H], U32) for h in both}
         o_scales = {h: tile("os%d" % h, [P, 2, H], U8) for h in both}
-        junk = tile("junk", [P, H], BF16)
         warm = tile("warm", [P, 16], F32)
 
         live = {}
@@ -103,7 +102,7 @@ def tile_epropeligibilityweightupdate_x2_kernel(
         def warmpe(n):
             b = bank()
             for k in range(n):
-                nc.tensor.matmul(b[:], lhsT=junk[:, 0:P], rhs=junk[:], start=True, stop=True)
+                nc.tensor.matmul(b[:, 0:P], lhsT=ident[:], rhs=ident[:], start=True, stop=True)
 
         def ld_z(g, j, a0=0, a1=2):
             src = rows(z, g)[:, 2 * j + a0 : 2 * j + a1, :].rearrange("p t c -> p (t c)")
@@ -112,11 +111,11 @@ def tile_epropeligibilityweightupdate_x2_kernel(
         def ld_e(g):
             nc.sync.dma_start(out=e_sb[g][:], in_=rows(err, g).rearrange("p t c -> p (t c)"))
 
-        def ld_v(g, h, t0=0, t1=4):
-            nc.sync.dma_start(out=v_sb[g, h][:, t0:t1, :], in_=rows(v0, g)[:, t0:t1, half(h)])
+        def ld_v(g, j, a0=0, a1=2):
+            nc.sync.dma_start(out=v_sb[g, j][:, a0:a1, :], in_=rows(v0, g)[:, 2 * j + a0 : 2 * j + a1, :])
 
-        def ld_zb(g, i):
-            nc.sync.dma_start(out=zb_sb[g, i][:], in_=rows(zbar, g)[:, :, half(i)])
+        def ld_zb(g, c0=0, c1=PRE):
+            nc.sync.dma_start(out=zb_sb[g][:, :, c0:c1], in_=rows(zbar, g)[:, :, c0:c1])
 
         def ld_w(h):
             src = wrec_words.rearrange("c p b -> p c b")[:, :, 2 * H * h : 2 * H * (h + 1)]
@@ -177,7 +176,7 @@ def tile_epropeligibilityweightupdate_x2_kernel(
         def addv(g, h, t):
             v = staged(("psi", g, h), 4, [P, 4, H], F32)
             nc.vector.scalar_tensor_tensor(
-                out=v[:, t, :], in0=v_sb[g, h][:, t, :], scalar=0.8,
+                out=v[:, t, :], in0=v_sb[g, t // 2][:, t % 2, half(h)], scalar=0.8,
                 in1=live.pop(("zw", g, h, t))[:], op0=ALU.mult, op1=ALU.add)
 
         def dist(g, h, t0, t1, c0=0, c1=H):
@@ -216,7 +215,7 @@ def tile_epropeligibilityweightupdate_x2_kernel(
         def zc(eng, g, i, m0=0, m1=P):
             grouped = staged(("zg", g, i), ZG, [P, 4, P, 4], BF16)
             copy(eng, grouped[:, :, m0:m1, :].rearrange("p s m t -> p m s t"),
-                 zb_sb[g, i][:].rearrange("p t (m s) -> p m s t", s=4)[:, m0:m1, :, :])
+                 zb_sb[g][:, :, half(i)].rearrange("p t (m s) -> p m s t", s=4)[:, m0:m1, :, :])
 
         def zq(g, i):
             nc.vector.quantize_mx(
@@ -243,7 +242,7 @@ def tile_epropeligibilityweightupdate_x2_kernel(
                  live.pop(("o", i, h, c0, k))[:].rearrange("p (a n) -> p a n", a=per))
 
         def oround(eng, i, h, c0, c1):
-            ob = staged(("ob", i, h), 2, [P, H, 4], BF16)
+            ob = staged(("ob", i, h), 4, [P, H, 4], BF16)
             copy(eng, ob[:, c0:c1, :].rearrange("p (c i) s -> p c s i", i=4),
                  o_f32[i, h][:, :, c0:c1].rearrange("p s (c i) -> p c s i", i=4))
 
@@ -270,157 +269,169 @@ def tile_epropeligibilityweightupdate_x2_kernel(
         ld_ws("S")
         ld_z(0, 1)
         ld_w(0)
-        ld_v(0, 0, 0, 2)
-        ld_v(0, 0, 2, 4)
+        ld_v(0, 0, 0, 1)
+        ld_v(0, 0, 1, 2)
+        ld_v(0, 1)
+        ld_w(1)
+        ld_zb(0, 0, H)
         ld_e(0)
         ld_bs("Y")
-        ld_z(1, 0)
-        ld_zb(0, 0)
         ld_b()
+        ld_z(1, 0)
+        ld_zb(0, H, PRE)
         ld_z(1, 1)
         ld_e(1)
         ld_v(1, 0)
-        ld_zb(1, 0)
-        ld_w(1)
-        ld_v(0, 1)
-        ld_zb(0, 1)
+        ld_zb(1)
         ld_v(1, 1)
-        ld_zb(1, 1)
+
+        def shape_psi(g, h):
+            dist(g, h, 0, 2)
+            dist(g, h, 2, 4)
+            ramp(g, h, 0, 4, 0, 256)
+            ramp(g, h, 0, 4, 256, 512)
+
+        def out_banks(h, c0):
+            for i in both:
+                for k in both:
+                    mo(i, h, c0, 256, k)
+
+        def out_copies(engs, h, c0):
+            for i in both:
+                for k in both:
+                    ocopy(engs[2 * i + k], i, h, c0, 256, k)
+                    st_f("Y", i, h, c0, c0 + 256, 2 * k, 2 * k + 2)
+
+        def planes(engs, h, c0):
+            for i in both:
+                oround(engs[i], i, h, c0, c0 + 256)
+            for i in both:
+                oq(i, h, c0, c0 + 256)
+                st_c("Y", i, h, c0, c0 + 256)
 
         warmact()
+        warmpe(2)
         for t in range(4):
             turn("z", 0, t)
             tcopy("S", "z", 0, t)
-            if t < 2:
-                tq("z", 0, 0, t, t + 1)
-        tq("z", 0, 1)
-        for t in range(4):
+            if t < 3:
+                tq("z", 0, t // 2, t % 2, t % 2 + 1)
+            if t == 1:
+                warmpe(2)
+        mz(0, 0, 0)
+        mz(0, 0, 1)
+        addv(0, 0, 0)
+        tq("z", 0, 1, 1, 2)
+        dist(0, 0, 0, 1)
+        addv(0, 0, 1)
+        dist(0, 0, 1, 2)
+        for t in (2, 3):
             mz(0, 0, t)
+            addv(0, 0, t)
+        for t in range(4):
+            mz(0, 1, t)
         for j in both:
             turn("e", 0, j)
-        for t in range(4):
-            addv(0, 0, t)
-            turn("z", 1, t)
-        dist(0, 0, 0, 2)
+        zc("G", 0, 0)
+        ramp(0, 0, 0, 2)
         dist(0, 0, 2, 4)
-        for j in both:
-            tcopy("V", "e", 0, j)
-        for t in (0, 1):
-            tcopy("S", "z", 1, t)
-        zc("V", 0, 0)
-        tq("e", 0, 0)
-        ramp(0, 0, 0, 4, 0, 256)
-        ramp(0, 0, 0, 4, 256, 512)
-        tq("z", 1, 0)
-        zq(0, 0)
-        for q in range(4):
-            ml(0, 0, q)
-        for t in (2, 3):
-            tcopy("S", "z", 1, t)
-        for j in both:
-            turn("e", 1, j)
-        for t in (0, 1):
-            mz(1, 0, t)
-        for q in range(3):
-            gate(0, 0, q)
-        for j in both:
-            tcopy("S", "e", 1, j)
-        tq("z", 1, 1)
-        gate(0, 0, 3)
-        for t in (2, 3):
-            mz(1, 0, t)
-        zc("S", 1, 0)
-        for t in range(4):
-            addv(1, 0, t)
-            mz(0, 1, t)
-        tq("e", 1, 0)
-        dq(0, 0)
-        zq(1, 0)
-        for q in range(4):
-            ml(1, 0, q)
-        dist(1, 0, 0, 2)
-        dist(1, 0, 2, 4)
-        ramp(1, 0, 0, 4, 0, 256)
-        ramp(1, 0, 0, 4, 256, 512)
         for t in range(4):
             addv(0, 1, t)
-            mz(1, 1, t)
+        for j in both:
+            tcopy("V", "e", 0, j)
+        ramp(0, 0, 2, 4)
+        tq("e", 0, 0)
+        zq(0, 0)
+        zc("G", 0, 1)
+        warmpe(2)
+        for t in (0, 1):
+            turn("z", 1, t)
         for q in range(4):
+            ml(0, 0, q)
+        dist(0, 1, 0, 2)
+        for t in (0, 1):
+            tcopy("S", "z", 1, t)
+        dist(0, 1, 2, 4)
+        for t in (2, 3):
+            turn("z", 1, t)
+            tcopy("S", "z", 1, t)
+        for q in range(4):
+            gate(0, 0, q)
+        for j in both:
+            turn("e", 1, j)
+        tq("z", 1, 0)
+        dq(0, 0)
+        tq("z", 1, 1)
+        zq(0, 1)
+        for t in range(4):
+            mz(1, 0, t)
+        zc("G", 1, 0)
+        ramp(0, 1, 0, 4, 0, 256)
+        ramp(0, 1, 0, 4, 256, 512)
+        for j in both:
+            tcopy("S", "e", 1, j)
+        for t in range(4):
+            addv(1, 0, t)
+            mz(1, 1, t)
+        shape_psi(1, 0)
+        tq("e", 1, 0)
+        zq(1, 0)
+        zc("G", 1, 1)
+        for q in range(4):
+            ml(1, 0, q)
+        for t in range(4):
+            addv(1, 1, t)
+        for q in (0, 1):
+            ml(0, 1, q)
+        gate(1, 0, 0)
+        gate(1, 0, 1)
+        zq(1, 1)
+        dq(1, 0, 0, 256)
+        for q in (2, 3):
             gate(1, 0, q)
             ml(0, 1, q)
-        zc("S", 0, 1)
-        dist(0, 1, 0, 2)
-        dist(0, 1, 2, 4)
-        addv(1, 1, 0)
-        dq(1, 0)
-        zq(0, 1)
-        for t in range(1, 4):
-            addv(1, 1, t)
-        for s in range(4):
-            mo(0, 0, 0, 512, s)
-        zc("V", 1, 1)
-        ramp(0, 1, 0, 4, 0, 256)
-        for s in range(4):
-            ocopy("S", 0, 0, 0, 512, s)
-            if s % 2:
-                st_f("Y", 0, 0, 0, 512, s - 1, s + 1)
-        ramp(0, 1, 0, 4, 256, 512)
-        gate(0, 1, 0)
-        zq(1, 1)
-        gate(0, 1, 1)
-        for s in range(4):
-            mo(1, 0, 0, 512, s)
-        dist(1, 1, 0, 4, 0, 256)
-        oround("V", 0, 0, 0, 512)
-        for q in (2, 3):
-            gate(0, 1, q)
-        for q in range(4):
-            ml(1, 1, q)
-        ocopy("S", 1, 0, 0, 512, 0)
+        out_banks(0, 0)
+        dist(1, 1, 0, 2)
+        dist(1, 1, 2, 4)
         ramp(1, 1, 0, 4, 0, 256)
-        oq(0, 0, 0, 512)
-        st_c("Y", 0, 0, 0, 512)
-        dq(0, 1)
-        for s in range(1, 4):
-            ocopy("S", 1, 0, 0, 512, s)
-            if s % 2:
-                st_f("Y", 1, 0, 0, 512, s - 1, s + 1)
+        gate(0, 1, 0)
+        dq(1, 0, 256, 512)
+        gate(0, 1, 1)
         for q in (0, 1):
-            gate(1, 1, q)
-        dist(1, 1, 0, 4, 256, 512)
-        oround("V", 1, 0, 0, 512)
-        dq(1, 1, 0, 256)
-        oq(1, 0, 0, 512)
-        st_c("Y", 1, 0, 0, 512)
-        for i in both:
-            for k in both:
-                mo(i, 1, 0, 256, k)
+            ml(1, 1, q)
+        out_copies("SSSS", 0, 0)
+        gate(0, 1, 2)
+        gate(0, 1, 3)
+        out_banks(0, 256)
         ramp(1, 1, 0, 4, 256, 512)
+        gate(1, 1, 0)
+        dq(0, 1)
+        gate(1, 1, 1)
+        for q in (2, 3):
+            ml(1, 1, q)
+        out_copies("SSSS", 0, 256)
+        oround("V", 0, 0, 0, 256)
+        dq(1, 1, 0, 256)
+        out_banks(1, 0)
+        gate(1, 1, 2)
+        gate(1, 1, 3)
+        oround("V", 1, 0, 0, 256)
+        dq(1, 1, 256, 512)
+        out_banks(1, 256)
+        out_copies("SSSS", 1, 0)
+        for i in both:
+            oround("V", i, 0, 256, 512)
+        out_copies("VSVS", 1, 256)
+        for i in both:
+            oq(i, 0, 0, 512)
+            st_c("Y", i, 0, 0, 512)
         for q in range(4):
             st_s("Y", 0, q)
-        for q in (2, 3):
-            gate(1, 1, q)
+        oround("S", 1, 1, 0, 256)
+        oround("V", 0, 1, 0, 512)
+        oround("S", 1, 1, 256, 512)
         for i in both:
-            for k in both:
-                ocopy("S", i, 1, 0, 256, k)
-            st_f("Y", i, 1, 0, 256)
-        oround("V", 0, 1, 0, 256)
-        dq(1, 1, 256, 512)
-        for i in both:
-            for k in both:
-                mo(i, 1, 256, 256, k)
-        oround("V", 1, 1, 0, 256)
-        for i in both:
-            oq(i, 1, 0, 256)
-            st_c("Y", i, 1, 0, 256)
-        for i in both:
-            for k in both:
-                ocopy("SV"[k], i, 1, 256, 256, k)
-            st_f("Y", i, 1, 256, 512)
-        for i in both:
-            oround("V", i, 1, 256, 512)
-        for i in both:
-            oq(i, 1, 256, 512)
-            st_c("Y", i, 1, 256, 512)
+            oq(i, 1, 0, 512)
+            st_c("Y", i, 1, 0, 512)
         for q in range(4):
             st_s("SY"[q % 2], 1, q)

@@ -18,7 +18,8 @@ ACT = mybir.ActivationFunctionType
 
 P = 128
 H = 512
-RUN = 4
+Q = 256
+RUN = 2
 ZG = 1
 
 
@@ -39,7 +40,10 @@ def tile_epropeligibilityweightupdate_x2_kernel(
         z_sb = {(g, j): tile("z%d%d" % (g, j), [P, 2 * PRE], BF16) for g in both for j in both}
         e_sb = {g: tile("e%d" % g, [P, 4 * O], BF16) for g in both}
         v_sb = {(g, j): tile("v%d%d" % (g, j), [P, 2, N], BF16) for g in both for j in both}
-        zb_sb = {g: tile("zb%d" % g, [P, 4, PRE], BF16) for g in both}
+        zb_sb = {(0, i): tile("zb0%d" % i, [P, 4, H], BF16) for i in both}
+        zb_whole = tile("zb1", [P, 4, PRE], BF16)
+        for i in both:
+            zb_sb[1, i] = zb_whole[:, :, H * i : H * (i + 1)]
         w_words = {h: tile("w%d" % h, [P, 2, 2 * H], U8) for h in both}
         b_words = tile("b_words", [P, 2 * N], U8)
         w_scales = tile("w_scales", [P, 2, N], U8)
@@ -52,7 +56,7 @@ def tile_epropeligibilityweightupdate_x2_kernel(
         zb_scales = {(g, i): tile("zbs%d%d" % (g, i), [P, H], U8) for g in both for i in both}
         d_codes = {(g, h): tile("dc%d%d" % (g, h), [P, H], U32) for g in both for h in both}
         d_scales = {(g, h): tile("ds%d%d" % (g, h), [P, H], U8) for g in both for h in both}
-        o_f32 = {(i, h): tile("of%d%d" % (i, h), [P, 4, H], F32) for i in both for h in both}
+        o_f32 = {(i, h, a): tile("of%d%d%d" % (i, h, a), [P, 4, Q], F32) for i in both for h in both for a in both}
         o_codes = {h: tile("oc%d" % h, [P, 2, H], U32) for h in both}
         o_scales = {h: tile("os%d" % h, [P, 2, H], U8) for h in both}
         warm = tile("warm", [P, 16], F32)
@@ -70,8 +74,17 @@ def tile_epropeligibilityweightupdate_x2_kernel(
                 live[key] = ring(keep, key[0], depth, shape, dtype, align_bytes=64)
             return live[key]
 
-        def bank():
-            return ring(psum, "bank", 8, [P, H], F32)
+        free = list(range(8))
+
+        def bank(key):
+            n = free.pop(0)
+            live[key] = (n, psum.tile([P, H], F32, name="bank%d" % n))
+            return live[key][1]
+
+        def drain(key):
+            n, b = live.pop(key)
+            free.append(n)
+            return b
 
         def rows(x, g):
             return x[512 * g : 512 * (g + 1), :].rearrange("(p t) c -> p t c", t=4)
@@ -100,9 +113,10 @@ def tile_epropeligibilityweightupdate_x2_kernel(
             nc.scalar.activation(out=warm[:, 8:9], in_=warm[:, 0:1], func=ACT.Abs)
 
         def warmpe(n):
-            b = bank()
+            b = bank("warm")
             for k in range(n):
                 nc.tensor.matmul(b[:, 0:P], lhsT=ident[:], rhs=ident[:], start=True, stop=True)
+            drain("warm")
 
         def ld_z(g, j, a0=0, a1=2):
             src = rows(z, g)[:, 2 * j + a0 : 2 * j + a1, :].rearrange("p t c -> p (t c)")
@@ -114,8 +128,11 @@ def tile_epropeligibilityweightupdate_x2_kernel(
         def ld_v(g, j, a0=0, a1=2):
             nc.sync.dma_start(out=v_sb[g, j][:, a0:a1, :], in_=rows(v0, g)[:, 2 * j + a0 : 2 * j + a1, :])
 
-        def ld_zb(g, c0=0, c1=PRE):
-            nc.sync.dma_start(out=zb_sb[g][:, :, c0:c1], in_=rows(zbar, g)[:, :, c0:c1])
+        def ld_zb(g, i=None):
+            if g == 0:
+                nc.sync.dma_start(out=zb_sb[0, i][:], in_=rows(zbar, 0)[:, :, half(i)])
+            else:
+                nc.sync.dma_start(out=zb_whole[:], in_=rows(zbar, 1))
 
         def ld_w(h):
             src = wrec_words.rearrange("c p b -> p c b")[:, :, 2 * H * h : 2 * H * (h + 1)]
@@ -143,18 +160,17 @@ def tile_epropeligibilityweightupdate_x2_kernel(
                 words = z_sb[g, j // 2][:, PRE * (j % 2) : PRE * (j % 2 + 1)].bitcast(F32)
             else:
                 words = e_sb[g][:, 2 * O * j : 2 * O * (j + 1)].bitcast(F32)
-            b = bank()
+            b = bank(("bank", kind, g, j))
             for a in both:
                 for u in both:
                     k = 2 * a + u
                     nc.tensor.transpose(b[:, P * k : P * (k + 1)], words[:, 2 * P * a + u : 2 * P * (a + 1) : 2], ident[:])
-            live["bank", kind, g, j] = b
 
         def tcopy(eng, kind, g, j):
             turned = staged(("turned", kind, g, j // 2), 3, [P, 2048], BF16)
             dst = turned[:, 1024 * (j % 2) : 1024 * (j % 2 + 1)].bitcast(F32)
             copy(eng, dst.rearrange("p (a m u) -> p a m u", a=2, u=2),
-                 live.pop(("bank", kind, g, j))[:].rearrange("p (a u m) -> p a m u", a=2, u=2))
+                 drain(("bank", kind, g, j))[:].rearrange("p (a u m) -> p a m u", a=2, u=2))
 
         def tq(kind, g, j, a0=0, a1=2):
             codes, scales = (z_codes[g, j], z_scales[g, j]) if kind == "z" else (e_codes[g], e_scales[g])
@@ -163,7 +179,7 @@ def tile_epropeligibilityweightupdate_x2_kernel(
                                   in_=live["turned", kind, g, j][:, 1024 * a0 : 1024 * a1])
 
         def mz(g, h, t):
-            b = bank()
+            b = bank(("zw", g, h, t))
             for c in both:
                 col = slice(P * (2 * (t % 2) + c), P * (2 * (t % 2) + c + 1))
                 nc.tensor.matmul_mx(
@@ -171,24 +187,23 @@ def tile_epropeligibilityweightupdate_x2_kernel(
                     lhsT=z_codes[g, t // 2][:, col].bitcast(FP8X4), lhsT_scale=z_scales[g, t // 2][:, col],
                     rhs=w_words[h][:, c, :].bitcast(FP4X4), rhs_scale=w_scales[:, c, half(h)],
                     start=(c == 0), stop=(c == 1))
-            live["zw", g, h, t] = b
 
         def addv(g, h, t):
-            v = staged(("psi", g, h), 4, [P, 4, H], F32)
+            v = staged(("psi", g, h), 4, [P, 2, 4, Q], F32)
             nc.vector.scalar_tensor_tensor(
-                out=v[:, t, :], in0=v_sb[g, t // 2][:, t % 2, half(h)], scalar=0.8,
-                in1=live.pop(("zw", g, h, t))[:], op0=ALU.mult, op1=ALU.add)
+                out=v[:, :, t, :], in0=v_sb[g, t // 2][:, t % 2, half(h)].rearrange("p (a n) -> p a n", a=2), scalar=0.8,
+                in1=drain(("zw", g, h, t))[:].rearrange("p (a n) -> p a n", a=2), op0=ALU.mult, op1=ALU.add)
 
         def dist(g, h, t0, t1, c0=0, c1=H):
-            v = live["psi", g, h][:, t0:t1, c0:c1]
+            v = live["psi", g, h][:, c0 // Q : c1 // Q, t0:t1, :]
             nc.scalar.activation(out=v, in_=v, func=ACT.Abs, bias=-1.0, scale=1.0)
 
         def ramp(g, h, t0, t1, c0=0, c1=H):
-            v = live["psi", g, h][:, t0:t1, c0:c1]
+            v = live["psi", g, h][:, c0 // Q : c1 // Q, t0:t1, :]
             nc.scalar.activation(out=v, in_=v, func=ACT.Relu, bias=0.3, scale=-0.3)
 
         def ml(g, h, q):
-            b = bank()
+            b = bank(("l", g, h, q))
             n0 = H * h + P * q
             for t in range(4):
                 nc.tensor.matmul_mx(
@@ -196,15 +211,14 @@ def tile_epropeligibilityweightupdate_x2_kernel(
                     lhsT=e_codes[g][:, P * t : P * (t + 1)].bitcast(FP8X4), lhsT_scale=e_scales[g][:, P * t : P * (t + 1)],
                     rhs=b_words[:, 2 * n0 : 2 * (n0 + P)].bitcast(FP4X4), rhs_scale=b_scales[:, n0 : n0 + P],
                     start=True, stop=True)
-            live["l", g, h, q] = b
 
         def gate(g, h, q):
             d = staged(("d", g, h), 3, [P, H, 4], BF16)
             cols = slice(P * q, P * (q + 1))
             nc.vector.tensor_tensor(
                 out=d[:, cols, :].rearrange("p (c i) t -> p c t i", i=RUN),
-                in0=live["psi", g, h][:, :, cols].rearrange("p t (c i) -> p c t i", i=RUN),
-                in1=live.pop(("l", g, h, q))[:].rearrange("p (t c i) -> p c t i", t=4, i=RUN),
+                in0=live["psi", g, h][:, q // 2, :, P * (q % 2) : P * (q % 2 + 1)].rearrange("p t (c i) -> p c t i", i=RUN),
+                in1=drain(("l", g, h, q))[:].rearrange("p (t c i) -> p c t i", t=4, i=RUN),
                 op=ALU.mult)
 
         def dq(g, h, c0=0, c1=H):
@@ -212,10 +226,10 @@ def tile_epropeligibilityweightupdate_x2_kernel(
                 out=d_codes[g, h][:, c0:c1].bitcast(FP8X4), scales=d_scales[g, h][:, c0:c1],
                 in_=live["d", g, h][:, c0:c1, :].rearrange("p n t -> p (n t)"))
 
-        def zc(eng, g, i, m0=0, m1=P):
+        def zc(eng, g, i, s0=0, s1=4):
             grouped = staged(("zg", g, i), ZG, [P, 4, P, 4], BF16)
-            copy(eng, grouped[:, :, m0:m1, :].rearrange("p s m t -> p m s t"),
-                 zb_sb[g][:, :, half(i)].rearrange("p t (m s) -> p m s t", s=4)[:, m0:m1, :, :])
+            copy(eng, grouped[:, s0:s1, :, :].rearrange("p s m t -> p m s t"),
+                 zb_sb[g, i][:].rearrange("p t (m s) -> p m s t", s=4)[:, :, s0:s1, :])
 
         def zq(g, i):
             nc.vector.quantize_mx(
@@ -223,7 +237,7 @@ def tile_epropeligibilityweightupdate_x2_kernel(
                 in_=live["zg", g, i][:].rearrange("p s m t -> p (s m t)"))
 
         def mo(i, h, c0, width, k):
-            b = bank()
+            b = bank(("o", i, h, c0, k))
             per = H // width
             c = slice(c0, c0 + width)
             for a in range(per):
@@ -234,17 +248,16 @@ def tile_epropeligibilityweightupdate_x2_kernel(
                         lhsT=zb_codes[g, i][:, P * s : P * (s + 1)].bitcast(FP8X4), lhsT_scale=zb_scales[g, i][:, P * s : P * (s + 1)],
                         rhs=d_codes[g, h][:, c].bitcast(FP8X4), rhs_scale=d_scales[g, h][:, c],
                         start=(g == 0), stop=(g == 1))
-            live["o", i, h, c0, k] = b
 
         def ocopy(eng, i, h, c0, width, k):
             per = H // width
-            copy(eng, o_f32[i, h][:, per * k : per * (k + 1), c0 : c0 + width],
-                 live.pop(("o", i, h, c0, k))[:].rearrange("p (a n) -> p a n", a=per))
+            copy(eng, o_f32[i, h, c0 // Q][:, per * k : per * (k + 1), :],
+                 drain(("o", i, h, c0, k))[:].rearrange("p (a n) -> p a n", a=per))
 
         def oround(eng, i, h, c0, c1):
             ob = staged(("ob", i, h), 4, [P, H, 4], BF16)
-            copy(eng, ob[:, c0:c1, :].rearrange("p (c i) s -> p c s i", i=4),
-                 o_f32[i, h][:, :, c0:c1].rearrange("p s (c i) -> p c s i", i=4))
+            copy(eng, ob[:, c0:c1, :].rearrange("p (c i) s -> p c s i", i=RUN),
+                 o_f32[i, h, c0 // Q][:].rearrange("p s (c i) -> p c s i", i=RUN))
 
         def oq(i, h, c0, c1):
             nc.vector.quantize_mx(
@@ -252,7 +265,7 @@ def tile_epropeligibilityweightupdate_x2_kernel(
                 in_=live["ob", i, h][:, c0:c1, :].rearrange("p n s -> p (n s)"))
 
         def st_f(eng, i, h, c0, c1, s0=0, s1=4):
-            queue(eng).dma_start(out=rows(out_0, i)[:, s0:s1, H * h + c0 : H * h + c1], in_=o_f32[i, h][:, s0:s1, c0:c1])
+            queue(eng).dma_start(out=rows(out_0, i)[:, s0:s1, H * h + c0 : H * h + c1], in_=o_f32[i, h, c0 // Q][:, s0:s1, :])
 
         def st_c(eng, i, h, c0, c1):
             dst = out_1[i].rearrange("p m t -> p (m t)").bitcast(I32)[:, H * h + c0 : H * h + c1]
@@ -263,22 +276,22 @@ def tile_epropeligibilityweightupdate_x2_kernel(
                 out=out_2[:, 4 * q : 4 * q + 4, half(h)].rearrange("g r n -> r g n").bitcast(I32),
                 in_=o_scales[h][32 * q : 32 * q + 4, :, :].bitcast(I32))
 
+        setup()
         ld_z(0, 0, 0, 1)
         ld_z(0, 0, 1, 2)
-        setup()
-        ld_ws("S")
+        ld_ws("Y")
         ld_z(0, 1)
         ld_w(0)
         ld_v(0, 0, 0, 1)
         ld_v(0, 0, 1, 2)
         ld_v(0, 1)
         ld_w(1)
-        ld_zb(0, 0, H)
+        ld_zb(0, 0)
         ld_e(0)
         ld_bs("Y")
         ld_b()
         ld_z(1, 0)
-        ld_zb(0, H, PRE)
+        ld_zb(0, 1)
         ld_z(1, 1)
         ld_e(1)
         ld_v(1, 0)
@@ -428,7 +441,8 @@ def tile_epropeligibilityweightupdate_x2_kernel(
         for q in range(4):
             st_s("Y", 0, q)
         oround("S", 1, 1, 0, 256)
-        oround("V", 0, 1, 0, 512)
+        oround("V", 0, 1, 0, 256)
+        oround("V", 0, 1, 256, 512)
         oround("S", 1, 1, 256, 512)
         for i in both:
             oq(i, 1, 0, 512)

@@ -20,6 +20,7 @@ P = 128
 H = 512
 Q = 256
 RUN = 2
+EARLY = False
 ZG = 1
 
 
@@ -58,7 +59,7 @@ def tile_epropeligibilityweightupdate_x2_kernel(
         d_scales = {(g, h): tile("ds%d%d" % (g, h), [P, H], U8) for g in both for h in both}
         o_f32 = {(i, h, a): tile("of%d%d%d" % (i, h, a), [P, 4, Q], F32) for i in both for h in both for a in both}
         o_codes = {h: tile("oc%d" % h, [P, 2, H], U32) for h in both}
-        o_scales = {h: tile("os%d" % h, [P, 2, H], U8) for h in both}
+        o_scales = tile("o_scales", [P, 2, N], U8)
         warm = tile("warm", [P, 16], F32)
 
         live = {}
@@ -167,7 +168,10 @@ def tile_epropeligibilityweightupdate_x2_kernel(
                     nc.tensor.transpose(b[:, P * k : P * (k + 1)], words[:, 2 * P * a + u : 2 * P * (a + 1) : 2], ident[:])
 
         def tcopy(eng, kind, g, j):
-            turned = staged(("turned", kind, g, j // 2), 3, [P, 2048], BF16)
+            key = ("turned", kind, g, j // 2)
+            if key not in live:
+                live[key] = tile("zg0" if key == ("turned", "e", 0, 0) and EARLY else "turned_%s%d%d" % key[1:], [P, 2048], BF16)
+            turned = live[key]
             dst = turned[:, 1024 * (j % 2) : 1024 * (j % 2 + 1)].bitcast(F32)
             copy(eng, dst.rearrange("p (a m u) -> p a m u", a=2, u=2),
                  drain(("bank", kind, g, j))[:].rearrange("p (a u m) -> p a m u", a=2, u=2))
@@ -213,7 +217,7 @@ def tile_epropeligibilityweightupdate_x2_kernel(
                     start=True, stop=True)
 
         def gate(g, h, q):
-            d = staged(("d", g, h), 3, [P, H, 4], BF16)
+            d = staged(("d", g, h), 4, [P, H, 4], BF16)
             cols = slice(P * q, P * (q + 1))
             nc.vector.tensor_tensor(
                 out=d[:, cols, :].rearrange("p (c i) t -> p c t i", i=RUN),
@@ -254,27 +258,32 @@ def tile_epropeligibilityweightupdate_x2_kernel(
             copy(eng, o_f32[i, h, c0 // Q][:, per * k : per * (k + 1), :],
                  drain(("o", i, h, c0, k))[:].rearrange("p (a n) -> p a n", a=per))
 
-        def oround(eng, i, h, c0, c1):
-            ob = staged(("ob", i, h), 4, [P, H, 4], BF16)
-            copy(eng, ob[:, c0:c1, :].rearrange("p (c i) s -> p c s i", i=RUN),
-                 o_f32[i, h, c0 // Q][:].rearrange("p s (c i) -> p c s i", i=RUN))
+        def oround(eng, i, h, c0, name=None):
+            ob = tile(name or "ob%d%d%d" % (i, h, c0 // Q), [P, Q, 4], BF16)
+            live["ob", i, h, c0] = ob
+            if eng == "G":
+                copy(eng, ob[:], o_f32[i, h, c0 // Q][:].rearrange("p s n -> p n s"))
+            else:
+                copy(eng, ob[:].rearrange("p (c i) s -> p c s i", i=RUN),
+                     o_f32[i, h, c0 // Q][:].rearrange("p s (c i) -> p c s i", i=RUN))
 
-        def oq(i, h, c0, c1):
+        def oq(i, h, c0):
+            c1 = c0 + Q
             nc.vector.quantize_mx(
-                out=o_codes[h][:, i, c0:c1].bitcast(FP8X4), scales=o_scales[h][:, i, c0:c1],
-                in_=live["ob", i, h][:, c0:c1, :].rearrange("p n s -> p (n s)"))
+                out=o_codes[h][:, i, c0:c1].bitcast(FP8X4), scales=o_scales[:, i, H * h + c0 : H * h + c1],
+                in_=live["ob", i, h, c0][:].rearrange("p n s -> p (n s)"))
 
         def st_f(eng, i, h, c0, c1, s0=0, s1=4):
             queue(eng).dma_start(out=rows(out_0, i)[:, s0:s1, H * h + c0 : H * h + c1], in_=o_f32[i, h, c0 // Q][:, s0:s1, :])
 
-        def st_c(eng, i, h, c0, c1):
-            dst = out_1[i].rearrange("p m t -> p (m t)").bitcast(I32)[:, H * h + c0 : H * h + c1]
-            queue(eng).dma_start(out=dst, in_=o_codes[h][:, i, c0:c1].bitcast(I32))
+        def st_c(h, c0, c1):
+            dst = out_1.rearrange("g p m t -> p g (m t)").bitcast(I32)[:, :, H * h + c0 : H * h + c1]
+            nc.sync.dma_start(out=dst, in_=o_codes[h][:, :, c0:c1].bitcast(I32))
 
-        def st_s(eng, h, q):
+        def st_s(eng, q):
             queue(eng).dma_start(
-                out=out_2[:, 4 * q : 4 * q + 4, half(h)].rearrange("g r n -> r g n").bitcast(I32),
-                in_=o_scales[h][32 * q : 32 * q + 4, :, :].bitcast(I32))
+                out=out_2[:, 4 * q : 4 * q + 4, :].rearrange("g r n -> r g n").bitcast(I32),
+                in_=o_scales[32 * q : 32 * q + 4, :, :].bitcast(I32))
 
         setup()
         ld_z(0, 0, 0, 1)
@@ -304,23 +313,17 @@ def tile_epropeligibilityweightupdate_x2_kernel(
             ramp(g, h, 0, 4, 0, 256)
             ramp(g, h, 0, 4, 256, 512)
 
-        def out_banks(h, c0):
-            for i in both:
-                for k in both:
-                    mo(i, h, c0, 256, k)
+        def out_banks(i, h, c0):
+            for k in both:
+                mo(i, h, c0, 256, k)
 
-        def out_copies(engs, h, c0):
-            for i in both:
-                for k in both:
-                    ocopy(engs[2 * i + k], i, h, c0, 256, k)
+        def out_copies(engs, i, h, c0, by_bank=True):
+            for k in both:
+                ocopy(engs[k], i, h, c0, 256, k)
+                if by_bank:
                     st_f("Y", i, h, c0, c0 + 256, 2 * k, 2 * k + 2)
-
-        def planes(engs, h, c0):
-            for i in both:
-                oround(engs[i], i, h, c0, c0 + 256)
-            for i in both:
-                oq(i, h, c0, c0 + 256)
-                st_c("Y", i, h, c0, c0 + 256)
+            if not by_bank:
+                st_f("Y", i, h, c0, c0 + 256)
 
         warmact()
         warmpe(2)
@@ -355,7 +358,7 @@ def tile_epropeligibilityweightupdate_x2_kernel(
         ramp(0, 0, 2, 4)
         tq("e", 0, 0)
         zq(0, 0)
-        zc("G", 0, 1)
+        zc("G", 0, 1, 0, 3)
         warmpe(2)
         for t in (0, 1):
             turn("z", 1, t)
@@ -373,16 +376,18 @@ def tile_epropeligibilityweightupdate_x2_kernel(
         for j in both:
             turn("e", 1, j)
         tq("z", 1, 0)
+        zc("V", 0, 1, 3, 4)
         dq(0, 0)
         tq("z", 1, 1)
         zq(0, 1)
         for t in range(4):
             mz(1, 0, t)
-        zc("G", 1, 0)
+        zc("G", 1, 0, 0, 3)
         ramp(0, 1, 0, 4, 0, 256)
         ramp(0, 1, 0, 4, 256, 512)
         for j in both:
             tcopy("S", "e", 1, j)
+        zc("S", 1, 0, 3, 4)
         for t in range(4):
             addv(1, 0, t)
             mz(1, 1, t)
@@ -403,7 +408,8 @@ def tile_epropeligibilityweightupdate_x2_kernel(
         for q in (2, 3):
             gate(1, 0, q)
             ml(0, 1, q)
-        out_banks(0, 0)
+        for i in both:
+            out_banks(i, 0, 0)
         dist(1, 1, 0, 2)
         dist(1, 1, 2, 4)
         ramp(1, 1, 0, 4, 0, 256)
@@ -412,40 +418,48 @@ def tile_epropeligibilityweightupdate_x2_kernel(
         gate(0, 1, 1)
         for q in (0, 1):
             ml(1, 1, q)
-        out_copies("SSSS", 0, 0)
+        for i in both:
+            out_copies("SS", i, 0, 0)
         gate(0, 1, 2)
         gate(0, 1, 3)
-        out_banks(0, 256)
+        for i in both:
+            out_banks(i, 0, Q)
         ramp(1, 1, 0, 4, 256, 512)
         gate(1, 1, 0)
         dq(0, 1)
         gate(1, 1, 1)
         for q in (2, 3):
             ml(1, 1, q)
-        out_copies("SSSS", 0, 256)
-        oround("V", 0, 0, 0, 256)
+        for i in both:
+            out_copies("SS", i, 0, Q)
+        oround("V", 0, 0, 0)
         dq(1, 1, 0, 256)
-        out_banks(1, 0)
+        for i in both:
+            out_banks(i, 1, 0)
         gate(1, 1, 2)
         gate(1, 1, 3)
-        oround("V", 1, 0, 0, 256)
+        oround("V", 1, 0, 0)
         dq(1, 1, 256, 512)
-        out_banks(1, 256)
-        out_copies("SSSS", 1, 0)
         for i in both:
-            oround("V", i, 0, 256, 512)
-        out_copies("VSVS", 1, 256)
+            out_copies("SS", i, 1, 0)
+            out_banks(i, 1, Q)
         for i in both:
-            oq(i, 0, 0, 512)
-            st_c("Y", i, 0, 0, 512)
+            oround("V", i, 0, Q)
+        for i in both:
+            out_copies("VS", i, 1, Q, False)
+        for i in both:
+            for c0 in (0, Q):
+                oq(i, 0, c0)
+        st_c(0, 0, H)
+        oround("S", 1, 1, 0)
+        oround("V", 0, 1, 0)
+        oround("V", 0, 1, Q)
+        oround("S", 1, 1, Q)
+        oq(0, 1, 0)
+        oq(1, 1, 0)
+        st_c(1, 0, Q)
+        oq(0, 1, Q)
+        oq(1, 1, Q)
+        st_c(1, Q, H)
         for q in range(4):
-            st_s("Y", 0, q)
-        oround("S", 1, 1, 0, 256)
-        oround("V", 0, 1, 0, 256)
-        oround("V", 0, 1, 256, 512)
-        oround("S", 1, 1, 256, 512)
-        for i in both:
-            oq(i, 1, 0, 512)
-            st_c("Y", i, 1, 0, 512)
-        for q in range(4):
-            st_s("SY"[q % 2], 1, q)
+            st_s("SSYY"[q], q)

@@ -59,7 +59,7 @@ def tile_epropeligibilityweightupdate_x2_kernel(
         d_scales = {(g, h): tile("ds%d%d" % (g, h), [P, H], U8) for g in both for h in both}
         o_f32 = {(i, h, a): tile("of%d%d%d" % (i, h, a), [P, 4, Q], F32) for i in both for h in both for a in both}
         o_codes = {h: tile("oc%d" % h, [P, 2, H], U32) for h in both}
-        o_scales = tile("o_scales", [P, 2, N], U8)
+        o_scales = tile("o_scales", [P, N], U8)
         warm = tile("warm", [P, 16], F32)
 
         live = {}
@@ -206,6 +206,18 @@ def tile_epropeligibilityweightupdate_x2_kernel(
             v = live["psi", g, h][:, c0 // Q : c1 // Q, t0:t1, :]
             nc.scalar.activation(out=v, in_=v, func=ACT.Relu, bias=0.3, scale=-0.3)
 
+        def ramp_g(g, h, a, name):
+            w = tile(name, [P, Q, 4], F32)
+            live["w", g, h, a] = w
+            nc.gpsimd.tensor_scalar(out=w[:], in0=live["psi", g, h][:, a, :, :].rearrange("p t n -> p n t"),
+                                    scalar1=-0.3, scalar2=0.3, op0=ALU.mult, op1=ALU.add)
+
+        def gate_w(g, h, q):
+            d = staged(("d", g, h), 4, [P, H, 4], BF16)
+            nc.vector.scalar_tensor_tensor(
+                out=d[:, P * q : P * (q + 1), :], in0=live["w", g, h, q // 2][:, P * (q % 2) : P * (q % 2 + 1), :], scalar=0.0,
+                in1=drain(("l", g, h, q))[:].rearrange("p (t n) -> p n t", t=4), op0=ALU.max, op1=ALU.mult)
+
         def ml(g, h, q):
             b = bank(("l", g, h, q))
             n0 = H * h + P * q
@@ -240,18 +252,16 @@ def tile_epropeligibilityweightupdate_x2_kernel(
                 out=zb_codes[g, i][:].bitcast(FP8X4), scales=zb_scales[g, i][:],
                 in_=live["zg", g, i][:].rearrange("p s m t -> p (s m t)"))
 
-        def mo(i, h, c0, width, k):
-            b = bank(("o", i, h, c0, k))
-            per = H // width
-            c = slice(c0, c0 + width)
-            for a in range(per):
-                s = per * k + a
-                for g in both:
-                    nc.tensor.matmul_mx(
-                        out=b[:, width * a : width * (a + 1)],
-                        lhsT=zb_codes[g, i][:, P * s : P * (s + 1)].bitcast(FP8X4), lhsT_scale=zb_scales[g, i][:, P * s : P * (s + 1)],
-                        rhs=d_codes[g, h][:, c].bitcast(FP8X4), rhs_scale=d_scales[g, h][:, c],
-                        start=(g == 0), stop=(g == 1))
+        def mo(i, h, c0, k, g):
+            b = bank(("o", i, h, c0, k)) if g == 0 else live["o", i, h, c0, k][1]
+            c = slice(c0, c0 + Q)
+            for a in both:
+                s = 2 * k + a
+                nc.tensor.matmul_mx(
+                    out=b[:, Q * a : Q * (a + 1)],
+                    lhsT=zb_codes[g, i][:, P * s : P * (s + 1)].bitcast(FP8X4), lhsT_scale=zb_scales[g, i][:, P * s : P * (s + 1)],
+                    rhs=d_codes[g, h][:, c].bitcast(FP8X4), rhs_scale=d_scales[g, h][:, c],
+                    start=(g == 0 and a == 0), stop=(g == 1 and a == 1))
 
         def ocopy(eng, i, h, c0, width, k):
             per = H // width
@@ -270,7 +280,7 @@ def tile_epropeligibilityweightupdate_x2_kernel(
         def oq(i, h, c0):
             c1 = c0 + Q
             nc.vector.quantize_mx(
-                out=o_codes[h][:, i, c0:c1].bitcast(FP8X4), scales=o_scales[:, i, H * h + c0 : H * h + c1],
+                out=o_codes[h][:, i, c0:c1].bitcast(FP8X4), scales=o_scales[4 * i :, H * h + c0 : H * h + c1],
                 in_=live["ob", i, h, c0][:].rearrange("p n s -> p (n s)"))
 
         def st_f(eng, i, h, c0, c1, s0=0, s1=4):
@@ -282,8 +292,8 @@ def tile_epropeligibilityweightupdate_x2_kernel(
 
         def st_s(eng, q):
             queue(eng).dma_start(
-                out=out_2[:, 4 * q : 4 * q + 4, :].rearrange("g r n -> r g n").bitcast(I32),
-                in_=o_scales[32 * q : 32 * q + 4, :, :].bitcast(I32))
+                out=out_2[:, 4 * q : 4 * q + 4, :].bitcast(I32),
+                in_=o_scales[32 * q : 32 * q + 8, :].bitcast(I32))
 
         setup()
         ld_z(0, 0, 0, 1)
@@ -315,7 +325,8 @@ def tile_epropeligibilityweightupdate_x2_kernel(
 
         def out_banks(i, h, c0):
             for k in both:
-                mo(i, h, c0, 256, k)
+                for g in both:
+                    mo(i, h, c0, k, g)
 
         def out_copies(engs, i, h, c0, by_bank=True):
             for k in both:
@@ -354,7 +365,7 @@ def tile_epropeligibilityweightupdate_x2_kernel(
         for t in range(4):
             addv(0, 1, t)
         for j in both:
-            tcopy("V", "e", 0, j)
+            tcopy("SV"[j], "e", 0, j)
         ramp(0, 0, 2, 4)
         tq("e", 0, 0)
         zq(0, 0)
@@ -384,69 +395,72 @@ def tile_epropeligibilityweightupdate_x2_kernel(
             mz(1, 0, t)
         zc("G", 1, 0, 0, 3)
         ramp(0, 1, 0, 4, 0, 256)
-        ramp(0, 1, 0, 4, 256, 512)
         for j in both:
             tcopy("S", "e", 1, j)
         zc("S", 1, 0, 3, 4)
         for t in range(4):
             addv(1, 0, t)
-            mz(1, 1, t)
+            mz(1, 1, 3 - t)
         shape_psi(1, 0)
         tq("e", 1, 0)
         zq(1, 0)
         zc("G", 1, 1)
-        for q in range(4):
+        for q in (3, 2, 1, 0):
             ml(1, 0, q)
         for t in range(4):
             addv(1, 1, t)
-        for q in (0, 1):
+        for q in (1, 0):
             ml(0, 1, q)
         gate(1, 0, 0)
         gate(1, 0, 1)
-        zq(1, 1)
+        gate(0, 1, 0)
         dq(1, 0, 0, 256)
+        zq(1, 1)
+        ramp_g(0, 1, 1, "zg0")
+        gate(0, 1, 1)
         for q in (2, 3):
             gate(1, 0, q)
             ml(0, 1, q)
-        for i in both:
-            out_banks(i, 0, 0)
+        for g in both:
+            for k in both:
+                mo(0, 0, 0, k, g)
+        out_banks(1, 0, 0)
         dist(1, 1, 0, 2)
         dist(1, 1, 2, 4)
         ramp(1, 1, 0, 4, 0, 256)
-        gate(0, 1, 0)
+        dq(0, 1, 0, Q)
         dq(1, 0, 256, 512)
-        gate(0, 1, 1)
-        for q in (0, 1):
+        ramp_g(1, 1, 1, "d1")
+        for q in (1, 0):
             ml(1, 1, q)
         for i in both:
             out_copies("SS", i, 0, 0)
-        gate(0, 1, 2)
-        gate(0, 1, 3)
+        gate(1, 1, 0)
+        gate(1, 1, 1)
         for i in both:
             out_banks(i, 0, Q)
-        ramp(1, 1, 0, 4, 256, 512)
-        gate(1, 1, 0)
-        dq(0, 1)
-        gate(1, 1, 1)
-        for q in (2, 3):
+        gate_w(0, 1, 2)
+        gate_w(0, 1, 3)
+        for q in (3, 2):
             ml(1, 1, q)
         for i in both:
             out_copies("SS", i, 0, Q)
-        oround("V", 0, 0, 0)
         dq(1, 1, 0, 256)
+        dq(0, 1, Q, H)
         for i in both:
             out_banks(i, 1, 0)
-        gate(1, 1, 2)
-        gate(1, 1, 3)
-        oround("V", 1, 0, 0)
+        gate_w(1, 1, 2)
+        gate_w(1, 1, 3)
+        oround("V", 0, 0, 0)
         dq(1, 1, 256, 512)
         for i in both:
             out_copies("SS", i, 1, 0)
             out_banks(i, 1, Q)
+        oround("V", 0, 0, Q)
+        for c0 in (0, Q):
+            oround("V", 1, 0, c0)
         for i in both:
-            oround("V", i, 0, Q)
-        for i in both:
-            out_copies("VS", i, 1, Q, False)
+            out_copies("SS", i, 1, Q, False)
         for i in both:
             for c0 in (0, Q):
                 oq(i, 0, c0)
@@ -456,9 +470,9 @@ def tile_epropeligibilityweightupdate_x2_kernel(
         oround("V", 0, 1, Q)
         oround("S", 1, 1, Q)
         oq(0, 1, 0)
+        oq(0, 1, Q)
         oq(1, 1, 0)
         st_c(1, 0, Q)
-        oq(0, 1, Q)
         oq(1, 1, Q)
         st_c(1, Q, H)
         for q in range(4):

@@ -336,15 +336,11 @@ def tile_epropeligibilityweightupdate_x2_kernel(
             if not by_bank:
                 st_f("Y", i, h, c0, c0 + 256)
 
-        warmact()
-        warmpe(2)
         for t in range(4):
             turn("z", 0, t)
             tcopy("S", "z", 0, t)
             if t < 3:
                 tq("z", 0, t // 2, t % 2, t % 2 + 1)
-            if t == 1:
-                warmpe(2)
         mz(0, 0, 0)
         mz(0, 0, 1)
         addv(0, 0, 0)
@@ -370,7 +366,6 @@ def tile_epropeligibilityweightupdate_x2_kernel(
         tq("e", 0, 0)
         zq(0, 0)
         zc("G", 0, 1, 0, 3)
-        warmpe(2)
         for t in (0, 1):
             turn("z", 1, t)
         for q in range(4):

@@ -41,13 +41,10 @@ def tile_epropeligibilityweightupdate_x2_kernel(
         z_sb = {(g, j): tile("z%d%d" % (g, j), [P, 2 * PRE], BF16) for g in both for j in both}
         e_sb = {g: tile("e%d" % g, [P, 4 * O], BF16) for g in both}
         v_sb = {(g, j): tile("v%d%d" % (g, j), [P, 2, N], BF16) for g in both for j in both}
-        zb_sb = {(0, i): tile("zb0%d" % i, [P, 4, H], BF16) for i in both}
-        zb_whole = tile("zb1", [P, 4, PRE], BF16)
-        for i in both:
-            zb_sb[1, i] = zb_whole[:, :, H * i : H * (i + 1)]
+        zb_sb = {(g, i): tile("zb%d%d" % (g, i), [P, 4, H], BF16) for g in both for i in both}
         w_words = {h: tile("w%d" % h, [P, 2, 2 * H], U8) for h in both}
         b_words = tile("b_words", [P, 2 * N], U8)
-        w_scales = tile("w_scales", [P, 2, N], U8)
+        w_scales = {h: tile("ws%d" % h, [P, 2, H], U8) for h in both}
         b_scales = tile("b_scales", [P, N], U8)
         z_codes = {(g, j): tile("zc%d%d" % (g, j), [P, 4 * P], U32) for g in both for j in both}
         z_scales = {(g, j): tile("zs%d%d" % (g, j), [P, 4 * P], U8) for g in both for j in both}
@@ -60,7 +57,6 @@ def tile_epropeligibilityweightupdate_x2_kernel(
         o_f32 = {(i, h, a): tile("of%d%d%d" % (i, h, a), [P, 4, Q], F32) for i in both for h in both for a in both}
         o_codes = {h: tile("oc%d" % h, [P, 2, H], U32) for h in both}
         o_scales = tile("o_scales", [P, N], U8)
-        warm = tile("warm", [P, 16], F32)
 
         live = {}
         count = {}
@@ -105,19 +101,10 @@ def tile_epropeligibilityweightupdate_x2_kernel(
             return {"S": nc.scalar, "G": nc.gpsimd, "Y": nc.sync}[eng]
 
         def setup():
-            nc.vector.memset(w_scales[:].rearrange("p c n -> p (c n)").bitcast(I32), 0)
+            for h in both:
+                nc.vector.memset(w_scales[h][:].rearrange("p c n -> p (c n)").bitcast(I32), 0)
             nc.vector.memset(b_scales[:].bitcast(I32), 0)
             make_identity(nc, ident[:])
-
-        def warmact():
-            nc.vector.memset(warm[:, 0:1], 0.0)
-            nc.scalar.activation(out=warm[:, 8:9], in_=warm[:, 0:1], func=ACT.Abs)
-
-        def warmpe(n):
-            b = bank("warm")
-            for k in range(n):
-                nc.tensor.matmul(b[:, 0:P], lhsT=ident[:], rhs=ident[:], start=True, stop=True)
-            drain("warm")
 
         def ld_z(g, j, a0=0, a1=2):
             src = rows(z, g)[:, 2 * j + a0 : 2 * j + a1, :].rearrange("p t c -> p (t c)")
@@ -129,11 +116,8 @@ def tile_epropeligibilityweightupdate_x2_kernel(
         def ld_v(g, j, a0=0, a1=2):
             nc.sync.dma_start(out=v_sb[g, j][:, a0:a1, :], in_=rows(v0, g)[:, 2 * j + a0 : 2 * j + a1, :])
 
-        def ld_zb(g, i=None):
-            if g == 0:
-                nc.sync.dma_start(out=zb_sb[0, i][:], in_=rows(zbar, 0)[:, :, half(i)])
-            else:
-                nc.sync.dma_start(out=zb_whole[:], in_=rows(zbar, 1))
+        def ld_zb(g, i):
+            nc.sync.dma_start(out=zb_sb[g, i][:], in_=rows(zbar, g)[:, :, half(i)])
 
         def ld_w(h):
             src = wrec_words.rearrange("c p b -> p c b")[:, :, 2 * H * h : 2 * H * (h + 1)]
@@ -142,19 +126,15 @@ def tile_epropeligibilityweightupdate_x2_kernel(
         def ld_b():
             nc.sync.dma_start(out=b_words[:].bitcast(I32), in_=bfb_words[0].bitcast(I32))
 
-        def ld_ws(eng):
-            for q in range(4):
-                queue(eng).dma_start(
-                    out=w_scales[32 * q : 32 * q + 4, :, :].bitcast(I32),
-                    in_=wrec_scales[:, 4 * q : 4 * q + 4, :].rearrange("c r n -> r c n").bitcast(I32),
-                )
+        def ld_ws(h):
+            for r in range(4):
+                nc.sync.dma_start(
+                    out=w_scales[h][r:P:32, :, :].bitcast(I32),
+                    in_=wrec_scales[:, r:16:4, half(h)].rearrange("c q n -> q c n").bitcast(I32))
 
-        def ld_bs(eng):
-            for q in range(4):
-                queue(eng).dma_start(
-                    out=b_scales[32 * q : 32 * q + 4, :].bitcast(I32),
-                    in_=bfb_scales[0, 4 * q : 4 * q + 4, :].bitcast(I32),
-                )
+        def ld_bs():
+            for r in range(4):
+                nc.sync.dma_start(out=b_scales[r:P:32, :].bitcast(I32), in_=bfb_scales[0, r:16:4, :].bitcast(I32))
 
         def turn(kind, g, j):
             if kind == "z":
@@ -189,7 +169,7 @@ def tile_epropeligibilityweightupdate_x2_kernel(
                 nc.tensor.matmul_mx(
                     out=b[:],
                     lhsT=z_codes[g, t // 2][:, col].bitcast(FP8X4), lhsT_scale=z_scales[g, t // 2][:, col],
-                    rhs=w_words[h][:, c, :].bitcast(FP4X4), rhs_scale=w_scales[:, c, half(h)],
+                    rhs=w_words[h][:, c, :].bitcast(FP4X4), rhs_scale=w_scales[h][:, c, :],
                     start=(c == 0), stop=(c == 1))
 
         def addv(g, h, t):
@@ -298,24 +278,25 @@ def tile_epropeligibilityweightupdate_x2_kernel(
         setup()
         ld_z(0, 0, 0, 1)
         ld_z(0, 0, 1, 2)
-        ld_ws("Y")
+        ld_ws(0)
         ld_z(0, 1)
         ld_w(0)
-        ld_v(0, 0, 0, 1)
-        ld_v(0, 0, 1, 2)
+        ld_v(0, 0)
         ld_v(0, 1)
+        ld_ws(1)
         ld_w(1)
         ld_zb(0, 0)
         ld_e(0)
-        ld_bs("Y")
+        ld_bs()
         ld_b()
         ld_z(1, 0)
         ld_zb(0, 1)
         ld_z(1, 1)
         ld_e(1)
         ld_v(1, 0)
-        ld_zb(1)
+        ld_zb(1, 0)
         ld_v(1, 1)
+        ld_zb(1, 1)
 
         def shape_psi(g, h):
             dist(g, h, 0, 2)

@@ -287,9 +287,9 @@ def tile_epropeligibilityweightupdate_x2_kernel(
         ld_w(1)
         ld_zb(0, 0)
         ld_e(0)
+        ld_z(1, 0)
         ld_bs()
         ld_b()
-        ld_z(1, 0)
         ld_zb(0, 1)
         ld_z(1, 1)
         ld_e(1)
@@ -448,8 +448,7 @@ def tile_epropeligibilityweightupdate_x2_kernel(
         oq(0, 1, 0)
         oq(0, 1, Q)
         oq(1, 1, 0)
-        st_c(1, 0, Q)
         oq(1, 1, Q)
-        st_c(1, Q, H)
+        st_c(1, 0, H)
         for q in range(4):
             st_s("SSYY"[q], q)

@@ -106,6 +106,12 @@ def tile_epropeligibilityweightupdate_x2_kernel(
             nc.vector.memset(b_scales[:].bitcast(I32), 0)
             make_identity(nc, ident[:])
 
+        def warmpe(n):
+            b = bank("warm")
+            for k in range(n):
+                nc.tensor.matmul(b[:, 0:P], lhsT=ident[:], rhs=ident[:], start=True, stop=True)
+            drain("warm")
+
         def ld_z(g, j, a0=0, a1=2):
             src = rows(z, g)[:, 2 * j + a0 : 2 * j + a1, :].rearrange("p t c -> p (t c)")
             nc.sync.dma_start(out=z_sb[g, j][:, PRE * a0 : PRE * a1], in_=src)
@@ -317,11 +323,14 @@ def tile_epropeligibilityweightupdate_x2_kernel(
             if not by_bank:
                 st_f("Y", i, h, c0, c0 + 256)
 
+        warmpe(2)
         for t in range(4):
             turn("z", 0, t)
             tcopy("S", "z", 0, t)
             if t < 3:
                 tq("z", 0, t // 2, t % 2, t % 2 + 1)
+            if t == 1:
+                warmpe(2)
         mz(0, 0, 0)
         mz(0, 0, 1)
         addv(0, 0, 0)
@@ -347,6 +356,7 @@ def tile_epropeligibilityweightupdate_x2_kernel(
         tq("e", 0, 0)
         zq(0, 0)
         zc("G", 0, 1, 0, 3)
+        warmpe(2)
         for t in (0, 1):
             turn("z", 1, t)
         for q in range(4):

@@ -38,6 +38,7 @@ def tile_epropeligibilityweightupdate_x2_kernel(
 
         both = range(2)
         ident = tile("ident", [P, P], F32)
+        zeros = tile("zeros", [P, H], BF16)
         z_sb = {(g, j): tile("z%d%d" % (g, j), [P, 2 * PRE], BF16) for g in both for j in both}
         e_sb = {g: tile("e%d" % g, [P, 4 * O], BF16) for g in both}
         v_sb = {(g, j): tile("v%d%d" % (g, j), [P, 2, N], BF16) for g in both for j in both}
@@ -101,6 +102,7 @@ def tile_epropeligibilityweightupdate_x2_kernel(
             return {"S": nc.scalar, "G": nc.gpsimd, "Y": nc.sync}[eng]
 
         def setup():
+            nc.vector.memset(zeros[:].bitcast(I32), 0)
             for h in both:
                 nc.vector.memset(w_scales[h][:].rearrange("p c n -> p (c n)").bitcast(I32), 0)
             nc.vector.memset(b_scales[:].bitcast(I32), 0)
@@ -109,7 +111,7 @@ def tile_epropeligibilityweightupdate_x2_kernel(
         def warmpe(n):
             b = bank("warm")
             for k in range(n):
-                nc.tensor.matmul(b[:, 0:P], lhsT=ident[:], rhs=ident[:], start=True, stop=True)
+                nc.tensor.matmul(b[:], lhsT=zeros[:, 0:P], rhs=zeros[:], start=True, stop=True)
             drain("warm")
 
         def ld_z(g, j, a0=0, a1=2):
@@ -255,19 +257,20 @@ def tile_epropeligibilityweightupdate_x2_kernel(
                  drain(("o", i, h, c0, k))[:].rearrange("p (a n) -> p a n", a=per))
 
         def oround(eng, i, h, c0, name=None):
-            ob = tile(name or "ob%d%d%d" % (i, h, c0 // Q), [P, Q, 4], BF16)
-            live["ob", i, h, c0] = ob
+            if ("ob", i, h) not in live:
+                live["ob", i, h] = tile("ob%d%d" % (i, h), [P, H, 4], BF16)
+            ob = live["ob", i, h][:, c0 : c0 + Q, :]
             if eng == "G":
-                copy(eng, ob[:], o_f32[i, h, c0 // Q][:].rearrange("p s n -> p n s"))
+                copy(eng, ob, o_f32[i, h, c0 // Q][:].rearrange("p s n -> p n s"))
             else:
-                copy(eng, ob[:].rearrange("p (c i) s -> p c s i", i=RUN),
+                copy(eng, ob.rearrange("p (c i) s -> p c s i", i=RUN),
                      o_f32[i, h, c0 // Q][:].rearrange("p s (c i) -> p c s i", i=RUN))
 
-        def oq(i, h, c0):
-            c1 = c0 + Q
+        def oq(i, h, c0, width=Q):
+            c1 = c0 + width
             nc.vector.quantize_mx(
                 out=o_codes[h][:, i, c0:c1].bitcast(FP8X4), scales=o_scales[4 * i :, H * h + c0 : H * h + c1],
-                in_=live["ob", i, h, c0][:].rearrange("p n s -> p (n s)"))
+                in_=live["ob", i, h][:, c0:c1, :].rearrange("p n s -> p (n s)"))
 
         def st_f(eng, i, h, c0, c1, s0=0, s1=4):
             queue(eng).dma_start(out=rows(out_0, i)[:, s0:s1, H * h + c0 : H * h + c1], in_=o_f32[i, h, c0 // Q][:, s0:s1, :])
@@ -323,7 +326,7 @@ def tile_epropeligibilityweightupdate_x2_kernel(
             if not by_bank:
                 st_f("Y", i, h, c0, c0 + 256)
 
-        warmpe(2)
+        warmpe(3)
         for t in range(4):
             turn("z", 0, t)
             tcopy("S", "z", 0, t)
@@ -377,7 +380,7 @@ def tile_epropeligibilityweightupdate_x2_kernel(
         dq(0, 0)
         tq("z", 1, 1)
         zq(0, 1)
-        for t in range(4):
+        for t in (1, 0, 3, 2):
             mz(1, 0, t)
         zc("G", 1, 0, 0, 3)
         ramp(0, 1, 0, 4, 0, 256)
@@ -399,10 +402,10 @@ def tile_epropeligibilityweightupdate_x2_kernel(
             ml(0, 1, q)
         gate(1, 0, 0)
         gate(1, 0, 1)
-        gate(0, 1, 0)
-        dq(1, 0, 0, 256)
         zq(1, 1)
+        dq(1, 0, 0, 256)
         ramp_g(0, 1, 1, "zg0")
+        gate(0, 1, 0)
         gate(0, 1, 1)
         for q in (2, 3):
             gate(1, 0, q)
@@ -413,14 +416,14 @@ def tile_epropeligibilityweightupdate_x2_kernel(
         out_banks(1, 0, 0)
         dist(1, 1, 0, 2)
         dist(1, 1, 2, 4)
-        ramp(1, 1, 0, 4, 0, 256)
         dq(0, 1, 0, Q)
         dq(1, 0, 256, 512)
         ramp_g(1, 1, 1, "d1")
         for q in (1, 0):
             ml(1, 1, q)
-        for i in both:
-            out_copies("SS", i, 0, 0)
+        out_copies("SS", 0, 0, 0)
+        ramp(1, 1, 0, 4, 0, 256)
+        out_copies("SS", 1, 0, 0)
         gate(1, 1, 0)
         gate(1, 1, 1)
         for i in both:
@@ -447,12 +450,11 @@ def tile_epropeligibilityweightupdate_x2_kernel(
             oround("V", 1, 0, c0)
         for i in both:
             out_copies("SS", i, 1, Q, False)
-        for i in both:
-            for c0 in (0, Q):
-                oq(i, 0, c0)
+        oq(0, 0, 0, H)
+        oround("V", 0, 1, 0)
+        oq(1, 0, 0, H)
         st_c(0, 0, H)
         oround("S", 1, 1, 0)
-        oround("V", 0, 1, 0)
         oround("V", 0, 1, Q)
         oround("S", 1, 1, Q)
         oq(0, 1, 0)

@@ -194,6 +194,10 @@ def tile_epropeligibilityweightupdate_x2_kernel(
             v = live["psi", g, h][:, c0 // Q : c1 // Q, t0:t1, :]
             nc.scalar.activation(out=v, in_=v, func=ACT.Relu, bias=0.3, scale=-0.3)
 
+        def ramp_part(g, h, a, k):
+            v = live["psi", g, h][:, a, :, P * k : P * (k + 1)]
+            nc.scalar.activation(out=v, in_=v, func=ACT.Relu, bias=0.3, scale=-0.3)
+
         def ramp_g(g, h, a, name):
             w = tile(name, [P, Q, 4], F32)
             live["w", g, h, a] = w
@@ -258,7 +262,7 @@ def tile_epropeligibilityweightupdate_x2_kernel(
 
         def oround(eng, i, h, c0, name=None):
             if ("ob", i, h) not in live:
-                live["ob", i, h] = tile("ob%d%d" % (i, h), [P, H, 4], BF16)
+                live["ob", i, h] = tile(name or "ob%d%d" % (i, h), [P, H, 4], BF16)
             ob = live["ob", i, h][:, c0 : c0 + Q, :]
             if eng == "G":
                 copy(eng, ob, o_f32[i, h, c0 // Q][:].rearrange("p s n -> p n s"))
@@ -278,6 +282,10 @@ def tile_epropeligibilityweightupdate_x2_kernel(
         def st_c(h, c0, c1):
             dst = out_1.rearrange("g p m t -> p g (m t)").bitcast(I32)[:, :, H * h + c0 : H * h + c1]
             nc.sync.dma_start(out=dst, in_=o_codes[h][:, :, c0:c1].bitcast(I32))
+
+        def st_ci(i, h, c0, c1):
+            dst = out_1[i].rearrange("p m t -> p (m t)").bitcast(I32)[:, H * h + c0 : H * h + c1]
+            nc.sync.dma_start(out=dst, in_=o_codes[h][:, i, c0:c1].bitcast(I32))
 
         def st_s(eng, q):
             queue(eng).dma_start(
@@ -405,24 +413,25 @@ def tile_epropeligibilityweightupdate_x2_kernel(
         zq(1, 1)
         dq(1, 0, 0, 256)
         ramp_g(0, 1, 1, "zg0")
-        gate(0, 1, 0)
-        gate(0, 1, 1)
         for q in (2, 3):
             gate(1, 0, q)
             ml(0, 1, q)
+        gate(0, 1, 0)
+        gate(0, 1, 1)
         for g in both:
             for k in both:
                 mo(0, 0, 0, k, g)
         out_banks(1, 0, 0)
         dist(1, 1, 0, 2)
         dist(1, 1, 2, 4)
-        dq(0, 1, 0, Q)
+        ramp_part(1, 1, 0, 0)
         dq(1, 0, 256, 512)
+        dq(0, 1, 0, Q)
         ramp_g(1, 1, 1, "d1")
         for q in (1, 0):
             ml(1, 1, q)
         out_copies("SS", 0, 0, 0)
-        ramp(1, 1, 0, 4, 0, 256)
+        ramp_part(1, 1, 0, 1)
         out_copies("SS", 1, 0, 0)
         gate(1, 1, 0)
         gate(1, 1, 1)
@@ -435,16 +444,16 @@ def tile_epropeligibilityweightupdate_x2_kernel(
         for i in both:
             out_copies("SS", i, 0, Q)
         dq(1, 1, 0, 256)
-        dq(0, 1, Q, H)
         for i in both:
             out_banks(i, 1, 0)
         gate_w(1, 1, 2)
         gate_w(1, 1, 3)
-        oround("V", 0, 0, 0)
+        dq(0, 1, Q, H)
         dq(1, 1, 256, 512)
         for i in both:
             out_copies("SS", i, 1, 0)
             out_banks(i, 1, Q)
+        oround("V", 0, 0, 0)
         oround("V", 0, 0, Q)
         for c0 in (0, Q):
             oround("V", 1, 0, c0)
@@ -459,8 +468,9 @@ def tile_epropeligibilityweightupdate_x2_kernel(
         oround("S", 1, 1, Q)
         oq(0, 1, 0)
         oq(0, 1, Q)
+        st_ci(0, 1, 0, H)
         oq(1, 1, 0)
         oq(1, 1, Q)
-        st_c(1, 0, H)
+        st_ci(1, 1, 0, H)
         for q in range(4):
             st_s("SSYY"[q], q)

@@ -194,10 +194,6 @@ def tile_epropeligibilityweightupdate_x2_kernel(
             v = live["psi", g, h][:, c0 // Q : c1 // Q, t0:t1, :]
             nc.scalar.activation(out=v, in_=v, func=ACT.Relu, bias=0.3, scale=-0.3)
 
-        def ramp_part(g, h, a, k):
-            v = live["psi", g, h][:, a, :, P * k : P * (k + 1)]
-            nc.scalar.activation(out=v, in_=v, func=ACT.Relu, bias=0.3, scale=-0.3)
-
         def ramp_g(g, h, a, name):
             w = tile(name, [P, Q, 4], F32)
             live["w", g, h, a] = w
@@ -315,12 +311,6 @@ def tile_epropeligibilityweightupdate_x2_kernel(
         ld_v(1, 1)
         ld_zb(1, 1)
 
-        def shape_psi(g, h):
-            dist(g, h, 0, 2)
-            dist(g, h, 2, 4)
-            ramp(g, h, 0, 4, 0, 256)
-            ramp(g, h, 0, 4, 256, 512)
-
         def out_banks(i, h, c0):
             for k in both:
                 for g in both:
@@ -362,14 +352,15 @@ def tile_epropeligibilityweightupdate_x2_kernel(
         for t in range(4):
             addv(0, 1, t)
         for j in both:
-            tcopy("SV"[j], "e", 0, j)
+            tcopy("V", "e", 0, j)
         ramp(0, 0, 2, 4)
-        tq("e", 0, 0)
+        for a in both:
+            tq("e", 0, 0, a, a + 1)
         zq(0, 0)
         zc("G", 0, 1, 0, 3)
-        warmpe(2)
         for t in (0, 1):
             turn("z", 1, t)
+        warmpe(1)
         for q in range(4):
             ml(0, 0, q)
         dist(0, 1, 0, 2)
@@ -388,7 +379,7 @@ def tile_epropeligibilityweightupdate_x2_kernel(
         dq(0, 0)
         tq("z", 1, 1)
         zq(0, 1)
-        for t in (1, 0, 3, 2):
+        for t in range(4):
             mz(1, 0, t)
         zc("G", 1, 0, 0, 3)
         ramp(0, 1, 0, 4, 0, 256)
@@ -398,7 +389,11 @@ def tile_epropeligibilityweightupdate_x2_kernel(
         for t in range(4):
             addv(1, 0, t)
             mz(1, 1, 3 - t)
-        shape_psi(1, 0)
+        for t in range(4):
+            dist(1, 0, t, t + 1)
+        for t in (0, 2):
+            ramp(1, 0, t, t + 2, 0, Q)
+        ramp(1, 0, 0, 4, Q, H)
         tq("e", 1, 0)
         zq(1, 0)
         zc("G", 1, 1)
@@ -417,30 +412,33 @@ def tile_epropeligibilityweightupdate_x2_kernel(
             gate(1, 0, q)
             ml(0, 1, q)
         gate(0, 1, 0)
-        gate(0, 1, 1)
         for g in both:
             for k in both:
                 mo(0, 0, 0, k, g)
         out_banks(1, 0, 0)
         dist(1, 1, 0, 2)
         dist(1, 1, 2, 4)
-        ramp_part(1, 1, 0, 0)
+        for t in (0, 2):
+            ramp(1, 1, t, t + 2, 0, Q)
+        out_copies("SS", 0, 0, 0)
+        gate(0, 1, 1)
         dq(1, 0, 256, 512)
         dq(0, 1, 0, Q)
         ramp_g(1, 1, 1, "d1")
-        for q in (1, 0):
+        for q in (0, 1):
             ml(1, 1, q)
-        out_copies("SS", 0, 0, 0)
-        ramp_part(1, 1, 0, 1)
         out_copies("SS", 1, 0, 0)
         gate(1, 1, 0)
         gate(1, 1, 1)
-        for i in both:
-            out_banks(i, 0, Q)
-        gate_w(0, 1, 2)
-        gate_w(0, 1, 3)
+        out_banks(0, 0, Q)
+        for g in both:
+            mo(1, 0, Q, 0, g)
         for q in (3, 2):
             ml(1, 1, q)
+        for g in both:
+            mo(1, 0, Q, 1, g)
+        gate_w(0, 1, 2)
+        gate_w(0, 1, 3)
         for i in both:
             out_copies("SS", i, 0, Q)
         dq(1, 1, 0, 256)

@@ -107,6 +107,7 @@ def tile_epropeligibilityweightupdate_x2_kernel(
                 nc.vector.memset(w_scales[h][:].rearrange("p c n -> p (c n)").bitcast(I32), 0)
             nc.vector.memset(b_scales[:].bitcast(I32), 0)
             make_identity(nc, ident[:])
+            nc.scalar.activation(out=tile("table_warm", [P, 16], F32)[:], in_=zeros[:, :16], func=ACT.Abs)
 
         def warmpe(n):
             b = bank("warm")
@@ -256,15 +257,12 @@ def tile_epropeligibilityweightupdate_x2_kernel(
             copy(eng, o_f32[i, h, c0 // Q][:, per * k : per * (k + 1), :],
                  drain(("o", i, h, c0, k))[:].rearrange("p (a n) -> p a n", a=per))
 
-        def oround(eng, i, h, c0, name=None):
+        def oround(eng, i, h, c0, w0=0, w1=Q, name=None):
             if ("ob", i, h) not in live:
                 live["ob", i, h] = tile(name or "ob%d%d" % (i, h), [P, H, 4], BF16)
-            ob = live["ob", i, h][:, c0 : c0 + Q, :]
-            if eng == "G":
-                copy(eng, ob, o_f32[i, h, c0 // Q][:].rearrange("p s n -> p n s"))
-            else:
-                copy(eng, ob.rearrange("p (c i) s -> p c s i", i=RUN),
-                     o_f32[i, h, c0 // Q][:].rearrange("p s (c i) -> p c s i", i=RUN))
+            ob = live["ob", i, h][:, c0 + w0 : c0 + w1, :]
+            copy(eng, ob.rearrange("p (c i) s -> p c s i", i=RUN),
+                 o_f32[i, h, c0 // Q][:, :, w0:w1].rearrange("p s (c i) -> p c s i", i=RUN))
 
         def oq(i, h, c0, width=Q):
             c1 = c0 + width
@@ -274,10 +272,6 @@ def tile_epropeligibilityweightupdate_x2_kernel(
 
         def st_f(eng, i, h, c0, c1, s0=0, s1=4):
             queue(eng).dma_start(out=rows(out_0, i)[:, s0:s1, H * h + c0 : H * h + c1], in_=o_f32[i, h, c0 // Q][:, s0:s1, :])
-
-        def st_c(h, c0, c1):
-            dst = out_1.rearrange("g p m t -> p g (m t)").bitcast(I32)[:, :, H * h + c0 : H * h + c1]
-            nc.sync.dma_start(out=dst, in_=o_codes[h][:, :, c0:c1].bitcast(I32))
 
         def st_ci(i, h, c0, c1):
             dst = out_1[i].rearrange("p m t -> p (m t)").bitcast(I32)[:, H * h + c0 : H * h + c1]
@@ -342,15 +336,17 @@ def tile_epropeligibilityweightupdate_x2_kernel(
         for t in (2, 3):
             mz(0, 0, t)
             addv(0, 0, t)
+        dist(0, 0, 2, 3)
         for t in range(4):
             mz(0, 1, t)
         for j in both:
             turn("e", 0, j)
         zc("G", 0, 0)
         ramp(0, 0, 0, 2)
-        dist(0, 0, 2, 4)
+        dist(0, 0, 3, 4)
         for t in range(4):
             addv(0, 1, t)
+        dist(0, 1, 0, 2)
         for j in both:
             tcopy("V", "e", 0, j)
         ramp(0, 0, 2, 4)
@@ -358,15 +354,15 @@ def tile_epropeligibilityweightupdate_x2_kernel(
             tq("e", 0, 0, a, a + 1)
         zq(0, 0)
         zc("G", 0, 1, 0, 3)
-        for t in (0, 1):
-            turn("z", 1, t)
         warmpe(1)
+        for t in both:
+            turn("z", 1, t)
         for q in range(4):
             ml(0, 0, q)
-        dist(0, 1, 0, 2)
-        for t in (0, 1):
-            tcopy("S", "z", 1, t)
         dist(0, 1, 2, 4)
+        for t in both:
+            tcopy("S", "z", 1, t)
+        ramp(0, 1, 0, 4, 0, Q)
         for t in (2, 3):
             turn("z", 1, t)
             tcopy("S", "z", 1, t)
@@ -382,65 +378,79 @@ def tile_epropeligibilityweightupdate_x2_kernel(
         for t in range(4):
             mz(1, 0, t)
         zc("G", 1, 0, 0, 3)
-        ramp(0, 1, 0, 4, 0, 256)
+        ramp(0, 1, 0, 4, Q, H)
         for j in both:
             tcopy("S", "e", 1, j)
         zc("S", 1, 0, 3, 4)
         for t in range(4):
             addv(1, 0, t)
-            mz(1, 1, 3 - t)
-        for t in range(4):
+            mz(1, 1, t)
+        for t in range(3):
             dist(1, 0, t, t + 1)
-        for t in (0, 2):
-            ramp(1, 0, t, t + 2, 0, Q)
-        ramp(1, 0, 0, 4, Q, H)
+        dist(1, 0, 3, 4, 0, Q)
+        ramp(1, 0, 0, 2, 0, Q)
+        ramp(1, 0, 2, 4, 0, Q)
+        dist(1, 0, 3, 4, Q, H)
+        ramp(1, 0, 0, 2, Q, H)
+        ramp(1, 0, 2, 4, Q, H)
         tq("e", 1, 0)
         zq(1, 0)
         zc("G", 1, 1)
-        for q in (3, 2, 1, 0):
+        for q in range(4):
             ml(1, 0, q)
-        for t in range(4):
-            addv(1, 1, t)
-        for q in (1, 0):
-            ml(0, 1, q)
-        gate(1, 0, 0)
-        gate(1, 0, 1)
+        for k in both:
+            addv(1, 1, k)
+            ml(0, 1, k)
+        addv(1, 1, 2)
+        mo(0, 0, 0, 0, 0)
+        for k in both:
+            gate(1, 0, k)
+            mo(k, 0, 0, 1 - k, 0)
+        addv(1, 1, 3)
+        mo(1, 0, 0, 1, 0)
+        dq(1, 0, 0, Q)
         zq(1, 1)
-        dq(1, 0, 0, 256)
-        ramp_g(0, 1, 1, "zg0")
-        for q in (2, 3):
-            gate(1, 0, q)
-            ml(0, 1, q)
-        gate(0, 1, 0)
-        for g in both:
-            for k in both:
-                mo(0, 0, 0, k, g)
-        out_banks(1, 0, 0)
         dist(1, 1, 0, 2)
-        dist(1, 1, 2, 4)
-        for t in (0, 2):
-            ramp(1, 1, t, t + 2, 0, Q)
+        for t in (2, 3):
+            dist(1, 1, t, t + 1, 0, Q)
+        dist(1, 1, 2, 4, Q, H)
+        ramp_g(1, 1, 0, "zg0")
+        for i in both:
+            for k in both:
+                mo(i, 0, 0, k, 1)
+        gate(1, 0, 2)
         out_copies("SS", 0, 0, 0)
-        gate(0, 1, 1)
-        dq(1, 0, 256, 512)
-        dq(0, 1, 0, Q)
-        ramp_g(1, 1, 1, "d1")
+        gate(1, 0, 3)
         for q in (0, 1):
             ml(1, 1, q)
+        gate(0, 1, 0)
         out_copies("SS", 1, 0, 0)
-        gate(1, 1, 0)
-        gate(1, 1, 1)
-        out_banks(0, 0, Q)
+        for q in (2, 3):
+            ml(0, 1, q)
+        gate(0, 1, 1)
+        dq(1, 0, Q, H)
+        dq(0, 1, 0, Q)
+        ramp_g(1, 1, 1, "d1")
+        oround("S", 0, 0, 0)
+        for g in both:
+            for k in both:
+                mo(0, 0, Q, k, g)
+        gate_w(1, 1, 0)
+        gate_w(1, 1, 1)
         for g in both:
             mo(1, 0, Q, 0, g)
-        for q in (3, 2):
+        for q in (2, 3):
             ml(1, 1, q)
         for g in both:
             mo(1, 0, Q, 1, g)
-        gate_w(0, 1, 2)
-        gate_w(0, 1, 3)
-        for i in both:
-            out_copies("SS", i, 0, Q)
+        gate(0, 1, 2)
+        gate(0, 1, 3)
+        out_copies("SS", 0, 0, Q)
+        for k in both:
+            ocopy("S", 1, 0, Q, Q, k)
+            st_f("Y", 1, 0, Q, H, 2 * k, 2 * k + 2)
+            if k == 0:
+                oround("S", 1, 0, 0, 0, P)
         dq(1, 1, 0, 256)
         for i in both:
             out_banks(i, 1, 0)
@@ -451,22 +461,24 @@ def tile_epropeligibilityweightupdate_x2_kernel(
         for i in both:
             out_copies("SS", i, 1, 0)
             out_banks(i, 1, Q)
-        oround("V", 0, 0, 0)
         oround("V", 0, 0, Q)
-        for c0 in (0, Q):
-            oround("V", 1, 0, c0)
+        oround("V", 1, 0, 0, P, Q)
+        oround("V", 1, 0, Q)
+        oq(0, 0, 0, H)
+        st_ci(0, 0, 0, H)
         for i in both:
             out_copies("SS", i, 1, Q, False)
-        oq(0, 0, 0, H)
         oround("V", 0, 1, 0)
         oq(1, 0, 0, H)
-        st_c(0, 0, H)
-        oround("S", 1, 1, 0)
+        st_ci(1, 0, 0, H)
+        oround("V", 1, 1, 0, P, Q)
         oround("V", 0, 1, Q)
-        oround("S", 1, 1, Q)
+        for c0 in (0, Q):
+            oround("S", 1, 1, c0, 0, P)
         oq(0, 1, 0)
         oq(0, 1, Q)
         st_ci(0, 1, 0, H)
+        oround("V", 1, 1, Q, P, Q)
         oq(1, 1, 0)
         oq(1, 1, Q)
         st_ci(1, 1, 0, H)

@@ -19,6 +19,7 @@ ACT = mybir.ActivationFunctionType
 P = 128
 H = 512
 Q = 256
+TAIL = 192
 RUN = 2
 EARLY = False
 ZG = 1
@@ -414,7 +415,7 @@ def tile_epropeligibilityweightupdate_x2_kernel(
         for t in (2, 3):
             dist(1, 1, t, t + 1, 0, Q)
         dist(1, 1, 2, 4, Q, H)
-        ramp_g(1, 1, 0, "zg0")
+        ramp_g(1, 1, 0, "turned_e10")
         for i in both:
             for k in both:
                 mo(i, 0, 0, k, 1)
@@ -471,10 +472,10 @@ def tile_epropeligibilityweightupdate_x2_kernel(
         oround("V", 0, 1, 0)
         oq(1, 0, 0, H)
         st_ci(1, 0, 0, H)
-        oround("V", 1, 1, 0, P, Q)
+        oround("V", 1, 1, 0, TAIL, Q)
         oround("V", 0, 1, Q)
-        for c0 in (0, Q):
-            oround("S", 1, 1, c0, 0, P)
+        oround("S", 1, 1, 0, 0, TAIL)
+        oround("S", 1, 1, Q, 0, P)
         oq(0, 1, 0)
         oq(0, 1, Q)
         st_ci(0, 1, 0, H)

from contextlib import ExitStack

import concourse.mybir as mybir
from concourse.masks import make_identity

M, PRE, N, O = 1024, 1024, 1024, 512
FLOPS = 2 * M * N * (PRE + O + PRE)

F32 = mybir.dt.float32
BF16 = mybir.dt.bfloat16
I32 = mybir.dt.int32
U32 = mybir.dt.uint32
U8 = mybir.dt.uint8
FP8X4 = mybir.dt.float8_e4m3fn_x4
FP4X4 = mybir.dt.float4_e2m1fn_x4
ALU = mybir.AluOpType
ACT = mybir.ActivationFunctionType

P = 128
H = 512
Q = 256
TAIL = 192
RUN = 2
EARLY = False
ZG = 1


def tile_epropeligibilityweightupdate_x2_kernel(
    tc, z, v0, wrec_words, wrec_scales, err, bfb_words, bfb_scales, zbar, out_0, out_1, out_2
):
    nc = tc.nc
    with ExitStack() as ctx:
        keep = ctx.enter_context(tc.tile_pool(name="keep", bufs=1))
        psum = ctx.enter_context(tc.psum_pool(name="psum", bufs=1))
        ctx.enter_context(tc.manual_schedule())

        def tile(name, shape, dtype):
            return keep.tile(shape, dtype, name=name, align_bytes=64)

        both = range(2)
        ident = tile("ident", [P, P], F32)
        zeros = tile("zeros", [P, H], BF16)
        z_sb = {(g, j): tile("z%d%d" % (g, j), [P, 2 * PRE], BF16) for g in both for j in both}
        e_sb = {g: tile("e%d" % g, [P, 4 * O], BF16) for g in both}
        v_sb = {(g, j): tile("v%d%d" % (g, j), [P, 2, N], BF16) for g in both for j in both}
        zb_sb = {(g, i): tile("zb%d%d" % (g, i), [P, 4, H], BF16) for g in both for i in both}
        w_words = {h: tile("w%d" % h, [P, 2, 2 * H], U8) for h in both}
        b_words = tile("b_words", [P, 2 * N], U8)
        w_scales = {h: tile("ws%d" % h, [P, 2, H], U8) for h in both}
        b_scales = tile("b_scales", [P, N], U8)
        z_codes = {(g, j): tile("zc%d%d" % (g, j), [P, 4 * P], U32) for g in both for j in both}
        z_scales = {(g, j): tile("zs%d%d" % (g, j), [P, 4 * P], U8) for g in both for j in both}
        e_codes = {g: tile("ec%d" % g, [P, 4 * P], U32) for g in both}
        e_scales = {g: tile("es%d" % g, [P, 4 * P], U8) for g in both}
        zb_codes = {(g, i): tile("zbc%d%d" % (g, i), [P, H], U32) for g in both for i in both}
        zb_scales = {(g, i): tile("zbs%d%d" % (g, i), [P, H], U8) for g in both for i in both}
        d_codes = {(g, h): tile("dc%d%d" % (g, h), [P, H], U32) for g in both for h in both}
        d_scales = {(g, h): tile("ds%d%d" % (g, h), [P, H], U8) for g in both for h in both}
        o_f32 = {(i, h, a): tile("of%d%d%d" % (i, h, a), [P, 4, Q], F32) for i in both for h in both for a in both}
        o_codes = {h: tile("oc%d" % h, [P, 2, H], U32) for h in both}
        o_scales = tile("o_scales", [P, N], U8)

        live = {}
        count = {}

        def ring(pool, name, depth, shape, dtype, **kw):
            n = count.get(name, 0)
            count[name] = n + 1
            return pool.tile(shape, dtype, name="%s%d" % (name, n % depth), **kw)

        def staged(key, depth, shape, dtype):
            if key not in live:
                live[key] = ring(keep, key[0], depth, shape, dtype, align_bytes=64)
            return live[key]

        free = list(range(8))

        def bank(key):
            n = free.pop(0)
            live[key] = (n, psum.tile([P, H], F32, name="bank%d" % n))
            return live[key][1]

        def drain(key):
            n, b = live.pop(key)
            free.append(n)
            return b

        def rows(x, g):
            return x[512 * g : 512 * (g + 1), :].rearrange("(p t) c -> p t c", t=4)

        def half(h):
            return slice(H * h, H * (h + 1))

        def copy(eng, out, in_):
            if eng == "S":
                nc.scalar.copy(out=out, in_=in_)
            elif eng == "V":
                nc.vector.tensor_copy(out=out, in_=in_)
            else:
                nc.gpsimd.tensor_scalar(out=out, in0=in_, scalar1=1.0, scalar2=0.0, op0=ALU.mult, op1=ALU.add)

        def queue(eng):
            return {"S": nc.scalar, "G": nc.gpsimd, "Y": nc.sync}[eng]

        def setup():
            nc.vector.memset(zeros[:].bitcast(I32), 0)
            for h in both:
                nc.vector.memset(w_scales[h][:].rearrange("p c n -> p (c n)").bitcast(I32), 0)
            nc.vector.memset(b_scales[:].bitcast(I32), 0)
            make_identity(nc, ident[:])
            nc.scalar.activation(out=tile("table_warm", [P, 16], F32)[:], in_=zeros[:, :16], func=ACT.Abs)

        def warmpe(n):
            b = bank("warm")
            for k in range(n):
                nc.tensor.matmul(b[:], lhsT=zeros[:, 0:P], rhs=zeros[:], start=True, stop=True)
            drain("warm")

        def ld_z(g, j, a0=0, a1=2):
            src = rows(z, g)[:, 2 * j + a0 : 2 * j + a1, :].rearrange("p t c -> p (t c)")
            nc.sync.dma_start(out=z_sb[g, j][:, PRE * a0 : PRE * a1], in_=src)

        def ld_e(g):
            nc.sync.dma_start(out=e_sb[g][:], in_=rows(err, g).rearrange("p t c -> p (t c)"))

        def ld_v(g, j, a0=0, a1=2):
            nc.sync.dma_start(out=v_sb[g, j][:, a0:a1, :], in_=rows(v0, g)[:, 2 * j + a0 : 2 * j + a1, :])

        def ld_zb(g, i):
            nc.sync.dma_start(out=zb_sb[g, i][:], in_=rows(zbar, g)[:, :, half(i)])

        def ld_w(h):
            src = wrec_words.rearrange("c p b -> p c b")[:, :, 2 * H * h : 2 * H * (h + 1)]
            nc.sync.dma_start(out=w_words[h][:].bitcast(I32), in_=src.bitcast(I32))

        def ld_b():
            nc.sync.dma_start(out=b_words[:].bitcast(I32), in_=bfb_words[0].bitcast(I32))

        def ld_ws(h):
            for r in range(4):
                nc.sync.dma_start(
                    out=w_scales[h][r:P:32, :, :].bitcast(I32),
                    in_=wrec_scales[:, r:16:4, half(h)].rearrange("c q n -> q c n").bitcast(I32))

        def ld_bs():
            for r in range(4):
                nc.sync.dma_start(out=b_scales[r:P:32, :].bitcast(I32), in_=bfb_scales[0, r:16:4, :].bitcast(I32))

        def turn(kind, g, j):
            if kind == "z":
                words = z_sb[g, j // 2][:, PRE * (j % 2) : PRE * (j % 2 + 1)].bitcast(F32)
            else:
                words = e_sb[g][:, 2 * O * j : 2 * O * (j + 1)].bitcast(F32)
            b = bank(("bank", kind, g, j))
            for a in both:
                for u in both:
                    k = 2 * a + u
                    nc.tensor.transpose(b[:, P * k : P * (k + 1)], words[:, 2 * P * a + u : 2 * P * (a + 1) : 2], ident[:])

        def tcopy(eng, kind, g, j):
            key = ("turned", kind, g, j // 2)
            if key not in live:
                live[key] = tile("zg0" if key == ("turned", "e", 0, 0) and EARLY else "turned_%s%d%d" % key[1:], [P, 2048], BF16)
            turned = live[key]
            dst = turned[:, 1024 * (j % 2) : 1024 * (j % 2 + 1)].bitcast(F32)
            copy(eng, dst.rearrange("p (a m u) -> p a m u", a=2, u=2),
                 drain(("bank", kind, g, j))[:].rearrange("p (a u m) -> p a m u", a=2, u=2))

        def tq(kind, g, j, a0=0, a1=2):
            codes, scales = (z_codes[g, j], z_scales[g, j]) if kind == "z" else (e_codes[g], e_scales[g])
            c = slice(256 * a0, 256 * a1)
            nc.vector.quantize_mx(out=codes[:, c].bitcast(FP8X4), scales=scales[:, c],
                                  in_=live["turned", kind, g, j][:, 1024 * a0 : 1024 * a1])

        def mz(g, h, t):
            b = bank(("zw", g, h, t))
            for c in both:
                col = slice(P * (2 * (t % 2) + c), P * (2 * (t % 2) + c + 1))
                nc.tensor.matmul_mx(
                    out=b[:],
                    lhsT=z_codes[g, t // 2][:, col].bitcast(FP8X4), lhsT_scale=z_scales[g, t // 2][:, col],
                    rhs=w_words[h][:, c, :].bitcast(FP4X4), rhs_scale=w_scales[h][:, c, :],
                    start=(c == 0), stop=(c == 1))

        def addv(g, h, t):
            v = staged(("psi", g, h), 4, [P, 2, 4, Q], F32)
            nc.vector.scalar_tensor_tensor(
                out=v[:, :, t, :], in0=v_sb[g, t // 2][:, t % 2, half(h)].rearrange("p (a n) -> p a n", a=2), scalar=0.8,
                in1=drain(("zw", g, h, t))[:].rearrange("p (a n) -> p a n", a=2), op0=ALU.mult, op1=ALU.add)

        def dist(g, h, t0, t1, c0=0, c1=H):
            v = live["psi", g, h][:, c0 // Q : c1 // Q, t0:t1, :]
            nc.scalar.activation(out=v, in_=v, func=ACT.Abs, bias=-1.0, scale=1.0)

        def ramp(g, h, t0, t1, c0=0, c1=H):
            v = live["psi", g, h][:, c0 // Q : c1 // Q, t0:t1, :]
            nc.scalar.activation(out=v, in_=v, func=ACT.Relu, bias=0.3, scale=-0.3)

        def ramp_g(g, h, a, name):
            w = tile(name, [P, Q, 4], F32)
            live["w", g, h, a] = w
            nc.gpsimd.tensor_scalar(out=w[:], in0=live["psi", g, h][:, a, :, :].rearrange("p t n -> p n t"),
                                    scalar1=-0.3, scalar2=0.3, op0=ALU.mult, op1=ALU.add)

        def gate_w(g, h, q):
            d = staged(("d", g, h), 4, [P, H, 4], BF16)
            nc.vector.scalar_tensor_tensor(
                out=d[:, P * q : P * (q + 1), :], in0=live["w", g, h, q // 2][:, P * (q % 2) : P * (q % 2 + 1), :], scalar=0.0,
                in1=drain(("l", g, h, q))[:].rearrange("p (t n) -> p n t", t=4), op0=ALU.max, op1=ALU.mult)

        def ml(g, h, q):
            b = bank(("l", g, h, q))
            n0 = H * h + P * q
            for t in range(4):
                nc.tensor.matmul_mx(
                    out=b[:, P * t : P * (t + 1)],
                    lhsT=e_codes[g][:, P * t : P * (t + 1)].bitcast(FP8X4), lhsT_scale=e_scales[g][:, P * t : P * (t + 1)],
                    rhs=b_words[:, 2 * n0 : 2 * (n0 + P)].bitcast(FP4X4), rhs_scale=b_scales[:, n0 : n0 + P],
                    start=True, stop=True)

        def gate(g, h, q):
            d = staged(("d", g, h), 4, [P, H, 4], BF16)
            cols = slice(P * q, P * (q + 1))
            nc.vector.tensor_tensor(
                out=d[:, cols, :].rearrange("p (c i) t -> p c t i", i=RUN),
                in0=live["psi", g, h][:, q // 2, :, P * (q % 2) : P * (q % 2 + 1)].rearrange("p t (c i) -> p c t i", i=RUN),
                in1=drain(("l", g, h, q))[:].rearrange("p (t c i) -> p c t i", t=4, i=RUN),
                op=ALU.mult)

        def dq(g, h, c0=0, c1=H):
            nc.vector.quantize_mx(
                out=d_codes[g, h][:, c0:c1].bitcast(FP8X4), scales=d_scales[g, h][:, c0:c1],
                in_=live["d", g, h][:, c0:c1, :].rearrange("p n t -> p (n t)"))

        def zc(eng, g, i, s0=0, s1=4):
            grouped = staged(("zg", g, i), ZG, [P, 4, P, 4], BF16)
            copy(eng, grouped[:, s0:s1, :, :].rearrange("p s m t -> p m s t"),
                 zb_sb[g, i][:].rearrange("p t (m s) -> p m s t", s=4)[:, :, s0:s1, :])

        def zq(g, i):
            nc.vector.quantize_mx(
                out=zb_codes[g, i][:].bitcast(FP8X4), scales=zb_scales[g, i][:],
                in_=live["zg", g, i][:].rearrange("p s m t -> p (s m t)"))

        def mo(i, h, c0, k, g):
            b = bank(("o", i, h, c0, k)) if g == 0 else live["o", i, h, c0, k][1]
            c = slice(c0, c0 + Q)
            for a in both:
                s = 2 * k + a
                nc.tensor.matmul_mx(
                    out=b[:, Q * a : Q * (a + 1)],
                    lhsT=zb_codes[g, i][:, P * s : P * (s + 1)].bitcast(FP8X4), lhsT_scale=zb_scales[g, i][:, P * s : P * (s + 1)],
                    rhs=d_codes[g, h][:, c].bitcast(FP8X4), rhs_scale=d_scales[g, h][:, c],
                    start=(g == 0 and a == 0), stop=(g == 1 and a == 1))

        def ocopy(eng, i, h, c0, width, k):
            per = H // width
            copy(eng, o_f32[i, h, c0 // Q][:, per * k : per * (k + 1), :],
                 drain(("o", i, h, c0, k))[:].rearrange("p (a n) -> p a n", a=per))

        def oround(eng, i, h, c0, w0=0, w1=Q, name=None):
            if ("ob", i, h) not in live:
                live["ob", i, h] = tile(name or "ob%d%d" % (i, h), [P, H, 4], BF16)
            ob = live["ob", i, h][:, c0 + w0 : c0 + w1, :]
            copy(eng, ob.rearrange("p (c i) s -> p c s i", i=RUN),
                 o_f32[i, h, c0 // Q][:, :, w0:w1].rearrange("p s (c i) -> p c s i", i=RUN))

        def oq(i, h, c0, width=Q):
            c1 = c0 + width
            nc.vector.quantize_mx(
                out=o_codes[h][:, i, c0:c1].bitcast(FP8X4), scales=o_scales[4 * i :, H * h + c0 : H * h + c1],
                in_=live["ob", i, h][:, c0:c1, :].rearrange("p n s -> p (n s)"))

        def st_f(eng, i, h, c0, c1, s0=0, s1=4):
            queue(eng).dma_start(out=rows(out_0, i)[:, s0:s1, H * h + c0 : H * h + c1], in_=o_f32[i, h, c0 // Q][:, s0:s1, :])

        def st_ci(i, h, c0, c1):
            dst = out_1[i].rearrange("p m t -> p (m t)").bitcast(I32)[:, H * h + c0 : H * h + c1]
            nc.sync.dma_start(out=dst, in_=o_codes[h][:, i, c0:c1].bitcast(I32))

        def st_s(eng, q):
            queue(eng).dma_start(
                out=out_2[:, 4 * q : 4 * q + 4, :].bitcast(I32),
                in_=o_scales[32 * q : 32 * q + 8, :].bitcast(I32))

        setup()
        ld_z(0, 0, 0, 1)
        ld_z(0, 0, 1, 2)
        ld_ws(0)
        ld_z(0, 1)
        ld_w(0)
        ld_v(0, 0)
        ld_v(0, 1)
        ld_ws(1)
        ld_w(1)
        ld_zb(0, 0)
        ld_e(0)
        ld_z(1, 0)
        ld_bs()
        ld_b()
        ld_zb(0, 1)
        ld_z(1, 1)
        ld_e(1)
        ld_v(1, 0)
        ld_zb(1, 0)
        ld_v(1, 1)
        ld_zb(1, 1)

        def out_banks(i, h, c0):
            for k in both:
                for g in both:
                    mo(i, h, c0, k, g)

        def out_copies(engs, i, h, c0, by_bank=True):
            for k in both:
                ocopy(engs[k], i, h, c0, 256, k)
                if by_bank:
                    st_f("Y", i, h, c0, c0 + 256, 2 * k, 2 * k + 2)
            if not by_bank:
                st_f("Y", i, h, c0, c0 + 256)

        warmpe(3)
        for t in range(4):
            turn("z", 0, t)
            tcopy("S", "z", 0, t)
            if t < 3:
                tq("z", 0, t // 2, t % 2, t % 2 + 1)
            if t == 1:
                warmpe(2)
        mz(0, 0, 0)
        mz(0, 0, 1)
        addv(0, 0, 0)
        tq("z", 0, 1, 1, 2)
        dist(0, 0, 0, 1)
        addv(0, 0, 1)
        dist(0, 0, 1, 2)
        for t in (2, 3):
            mz(0, 0, t)
            addv(0, 0, t)
        dist(0, 0, 2, 3)
        for t in range(4):
            mz(0, 1, t)
        for j in both:
            turn("e", 0, j)
        zc("G", 0, 0)
        ramp(0, 0, 0, 2)
        dist(0, 0, 3, 4)
        for t in range(4):
            addv(0, 1, t)
        dist(0, 1, 0, 2)
        for j in both:
            tcopy("V", "e", 0, j)
        ramp(0, 0, 2, 4)
        for a in both:
            tq("e", 0, 0, a, a + 1)
        zq(0, 0)
        zc("G", 0, 1, 0, 3)
        warmpe(1)
        for t in both:
            turn("z", 1, t)
        for q in range(4):
            ml(0, 0, q)
        dist(0, 1, 2, 4)
        for t in both:
            tcopy("S", "z", 1, t)
        ramp(0, 1, 0, 4, 0, Q)
        for t in (2, 3):
            turn("z", 1, t)
            tcopy("S", "z", 1, t)
        for q in range(4):
            gate(0, 0, q)
        for j in both:
            turn("e", 1, j)
        tq("z", 1, 0)
        zc("V", 0, 1, 3, 4)
        dq(0, 0)
        tq("z", 1, 1)
        zq(0, 1)
        for t in range(4):
            mz(1, 0, t)
        zc("G", 1, 0, 0, 3)
        ramp(0, 1, 0, 4, Q, H)
        for j in both:
            tcopy("S", "e", 1, j)
        zc("S", 1, 0, 3, 4)
        for t in range(4):
            addv(1, 0, t)
            mz(1, 1, t)
        for t in range(3):
            dist(1, 0, t, t + 1)
        dist(1, 0, 3, 4, 0, Q)
        ramp(1, 0, 0, 2, 0, Q)
        ramp(1, 0, 2, 4, 0, Q)
        dist(1, 0, 3, 4, Q, H)
        ramp(1, 0, 0, 2, Q, H)
        ramp(1, 0, 2, 4, Q, H)
        tq("e", 1, 0)
        zq(1, 0)
        zc("G", 1, 1)
        for q in range(4):
            ml(1, 0, q)
        for k in both:
            addv(1, 1, k)
            ml(0, 1, k)
        addv(1, 1, 2)
        mo(0, 0, 0, 0, 0)
        for k in both:
            gate(1, 0, k)
            mo(k, 0, 0, 1 - k, 0)
        addv(1, 1, 3)
        mo(1, 0, 0, 1, 0)
        dq(1, 0, 0, Q)
        zq(1, 1)
        dist(1, 1, 0, 2)
        for t in (2, 3):
            dist(1, 1, t, t + 1, 0, Q)
        dist(1, 1, 2, 4, Q, H)
        ramp_g(1, 1, 0, "turned_e10")
        for i in both:
            for k in both:
                mo(i, 0, 0, k, 1)
        gate(1, 0, 2)
        out_copies("SS", 0, 0, 0)
        gate(1, 0, 3)
        for q in (0, 1):
            ml(1, 1, q)
        gate(0, 1, 0)
        out_copies("SS", 1, 0, 0)
        for q in (2, 3):
            ml(0, 1, q)
        gate(0, 1, 1)
        dq(1, 0, Q, H)
        dq(0, 1, 0, Q)
        ramp_g(1, 1, 1, "d1")
        oround("S", 0, 0, 0)
        for g in both:
            for k in both:
                mo(0, 0, Q, k, g)
        gate_w(1, 1, 0)
        gate_w(1, 1, 1)
        for g in both:
            mo(1, 0, Q, 0, g)
        for q in (2, 3):
            ml(1, 1, q)
        for g in both:
            mo(1, 0, Q, 1, g)
        gate(0, 1, 2)
        gate(0, 1, 3)
        out_copies("SS", 0, 0, Q)
        for k in both:
            ocopy("S", 1, 0, Q, Q, k)
            st_f("Y", 1, 0, Q, H, 2 * k, 2 * k + 2)
            if k == 0:
                oround("S", 1, 0, 0, 0, P)
        dq(1, 1, 0, 256)
        for i in both:
            out_banks(i, 1, 0)
        gate_w(1, 1, 2)
        gate_w(1, 1, 3)
        dq(0, 1, Q, H)
        dq(1, 1, 256, 512)
        for i in both:
            out_copies("SS", i, 1, 0)
            out_banks(i, 1, Q)
        oround("V", 0, 0, Q)
        oround("V", 1, 0, 0, P, Q)
        oround("V", 1, 0, Q)
        oq(0, 0, 0, H)
        st_ci(0, 0, 0, H)
        for i in both:
            out_copies("SS", i, 1, Q, False)
        oround("V", 0, 1, 0)
        oq(1, 0, 0, H)
        st_ci(1, 0, 0, H)
        oround("V", 1, 1, 0, TAIL, Q)
        oround("V", 0, 1, Q)
        oround("S", 1, 1, 0, 0, TAIL)
        oround("S", 1, 1, Q, 0, P)
        oq(0, 1, 0)
        oq(0, 1, Q)
        st_ci(0, 1, 0, H)
        oround("V", 1, 1, Q, P, Q)
        oq(1, 1, 0)
        oq(1, 1, Q)
        st_ci(1, 1, 0, H)
        for q in range(4):
            st_s("SSYY"[q], q)
